import numpy as np
import ml_dtypes


def mxq(x, axis, fmt="e4m3"):
    dtype, down = {"e4m3": (ml_dtypes.float8_e4m3fn, 7), "e5m2": (ml_dtypes.float8_e5m2, 14)}[fmt]
    v = np.moveaxis(np.asarray(x, np.float32).astype(ml_dtypes.bfloat16).astype(np.float64), axis, -1)
    blocks = v.reshape(v.shape[:-1] + (-1, 32))
    amax = np.abs(blocks).max(-1, keepdims=True)
    byte = np.maximum(np.where(amax > 0, np.frexp(amax)[1] - 1 + 127, 0) - down, 1)
    scale = np.exp2(byte - 127.0)
    codes = (blocks / scale).astype(np.float32).astype(dtype).astype(np.float64)
    return np.moveaxis((codes * scale).reshape(v.shape), -1, axis)


WIDE = False


def mx_kscale(k):
    if not WIDE:
        return np.ones(k)
    levels = np.array([10, -10, 5, -5, 0])
    if k % 512:
        return np.exp2(np.random.permutation(np.resize(levels, k // 32))).repeat(32)
    a = np.empty((k // 512, 16))
    for p in range(k // 512):
        a[p, :8] = np.random.permutation(np.resize(levels, 8))
        for g in range(8):
            far = levels[np.abs(levels - a[p, g]) >= 10]
            a[p, g + 8] = far[np.random.randint(len(far))]
    return np.exp2(a.ravel()).repeat(32)


def f64(x):
    return np.asarray(x).astype(np.float64)


def striped(idx):
    return np.tile(idx.reshape(-1, 16).T, (8, 1)).astype(np.uint16)


def unstriped(offs):
    return offs[:16].T.reshape(-1).astype(np.int64)


def pack_weight(w):
    k, n = w.shape
    w = f64(np.asarray(w, np.float32).astype(ml_dtypes.bfloat16)).reshape(k // 32, 32, n)
    amax = np.abs(w).max(1)
    byte = np.clip(np.where(amax > 0, np.frexp(amax)[1] - 1 + 127 - 7, 1), 1, 254)
    scaled = (w * np.exp2(127.0 - byte)[:, None, :]).reshape(k, n).astype(np.float32)
    words = np.ascontiguousarray(scaled.reshape(k // 512, 128, 4, n).transpose(0, 1, 3, 2)).astype(ml_dtypes.float8_e4m3fn).view(np.uint8)
    return words, np.ascontiguousarray(byte.astype(np.uint8).reshape(k // 512, 16, n))


def unpack_weight(words, scales):
    g, p, n, _ = words.shape
    vals = np.ascontiguousarray(words).view(ml_dtypes.float8_e4m3fn).astype(np.float64) * np.repeat(np.exp2(scales.astype(np.float64) - 127.0), 8, axis=1)[..., None]
    return vals.transpose(0, 1, 3, 2).reshape(g * 512, n)


def gelu(v):
    return 0.5 * v * (1.0 + np.tanh(np.sqrt(2.0 / np.pi) * (v + 0.044715 * v**3)))


K, T, S, V, H, N, J = 1024, 2048, 1024, 512, 512, 128, 512


def setup_inputs():
    n = np.random.standard_normal
    s = mx_kscale(K)[:, None]
    u = mx_kscale(H)
    r = mx_kscale(J)[:, None]
    packed_xT = pack_weight(n((K, T)) * s)
    return {
        "x_words": packed_xT[0],
        "x_scales": packed_xT[1],
        "eT": (n((J, V)) * r).astype(np.float32),
        "w1": (n((K, H)) / np.sqrt(3 * K) / s * u).astype(np.float32),
        "w2": (n((K, H)) / np.sqrt(3 * K) / s * u).astype(np.float32),
        "w3": (n((J, H)) / np.sqrt(3 * J) / r * u).astype(np.float32),
        "w4": (n((H, N)) / np.sqrt(H) / u[:, None]).astype(np.float32),
        "offs": striped(np.random.permutation(T)[:S]),
    }


def reference(x_words, x_scales, eT, w1, w2, w3, w4, offs):
    xq = unpack_weight(x_words, x_scales)[:, unstriped(offs)]
    h = gelu(mxq(f64(w1), 0, "e4m3").T @ xq[:, :V] + mxq(f64(w2), 0, "e4m3").T @ xq[:, V:2 * V] + mxq(f64(w3), 0, "e4m3").T @ mxq(f64(eT), 0, "e4m3"))
    return mxq(f64(w4), 0, "e4m3").T @ mxq(h, 0, "e4m3")

@@ -1,0 +1,144 @@
+from contextlib import ExitStack
+
+import concourse.mybir as mybir
+
+K, T, V, H, N, J = 1024, 2048, 512, 512, 128, 512
+FLOPS = 2 * V * (2 * K * H + J * H + H * N)
+
+F32 = mybir.dt.float32
+BF16 = mybir.dt.bfloat16
+I32 = mybir.dt.int32
+U32 = mybir.dt.uint32
+U16 = mybir.dt.uint16
+U8 = mybir.dt.uint8
+FP8X4 = mybir.dt.float8_e4m3fn_x4
+GELU = mybir.ActivationFunctionType.Gelu_apprx_tanh
+
+P = 128
+PACK = 4
+K_PASS = P * PACK
+CHUNK = 128
+N_CHUNKS = V // CHUNK
+OFFS_COLS = V // 16
+
+
+def tile_picked_edgeup_gelu_p_kernel(tc, x_words, x_scales, eT, w1, w2, w3, w4, offs, out):
+    nc = tc.nc
+    with ExitStack() as ctx:
+        sb = ctx.enter_context(tc.tile_pool(name="sb", bufs=1))
+        ps = ctx.enter_context(tc.psum_pool(name="ps", bufs=1))
+
+        offsets = sb.tile([P, 2 * OFFS_COLS], U16, name="offsets")
+        nc.sync.dma_start(offsets[:], offs)
+
+        scale_table = sb.tile([P, T], U8, name="scale_table", align_bytes=64)
+        nc.vector.memset(scale_table[:].bitcast(I32), 0)
+        zero = sb.tile([P, 1], F32, name="zero")
+        nc.vector.memset(zero[:], 0.0)
+        gelu_bias = sb.tile([P, 1], F32, name="gelu_bias")
+
+        word_tables = [sb.tile([P, T], I32, name="word_table%d" % z, align_bytes=64) for z in range(2)]
+        nc.sync.dma_start(word_tables[0][:], x_words[0].rearrange("p n r -> p (n r)").bitcast(I32))
+        for q in range(4):
+            nc.scalar.dma_start(scale_table[32 * q : 32 * q + 8, :].bitcast(I32), x_scales[:, 4 * q : 4 * q + 4, :].bitcast(I32))
+        nc.scalar.activation(gelu_bias[:], zero[:], GELU)
+        nc.sync.dma_start(word_tables[1][:], x_words[1].rearrange("p n r -> p (n r)").bitcast(I32))
+
+        first_rows = [w1[0:K_PASS, :], w2[0:K_PASS, :], w1[K_PASS:K, :], w2[K_PASS:K, :], w3]
+        w_raw = []
+        for g, rows in enumerate(first_rows):
+            raw = sb.tile([P, PACK, H], F32, name="w_raw%d" % g)
+            nc.sync.dma_start(raw[:], rows.rearrange("(p j) c -> p j c", j=PACK))
+            w_raw.append(raw)
+        e_raw = []
+        for c in range(N_CHUNKS):
+            raw = sb.tile([P, PACK, CHUNK], F32, name="e_raw%d" % c)
+            nc.sync.dma_start(raw[:], eT[:, c * CHUNK : (c + 1) * CHUNK].rearrange("(p j) c -> p j c", j=PACK))
+            e_raw.append(raw)
+        w4_raw = sb.tile([P, PACK, N], F32, name="w4_raw")
+        nc.sync.dma_start(w4_raw[:], w4.rearrange("(p j) c -> p j c", j=PACK))
+
+        def gather_words(z, side):
+            picked = sb.tile([P, V], U32, name="x_codes%d%d" % (z, side), align_bytes=64)
+            nc.vector.tensor_copy(picked[:], word_tables[z][:].bitcast(U32).indirect(offsets[:, side * OFFS_COLS : (side + 1) * OFFS_COLS]))
+            return picked
+
+        x_codes = {}
+        x_codes[0, 0] = gather_words(0, 0)
+        x_codes[0, 1] = gather_words(0, 1)
+        x_planes = sb.tile([P, 2 * V], U8, name="x_planes", align_bytes=64)
+        nc.vector.tensor_copy(x_planes[:], scale_table[:].indirect(offsets[:]))
+        x_codes[1, 0] = gather_words(1, 0)
+        x_codes[1, 1] = gather_words(1, 1)
+
+        def quantize(grouped, width, name):
+            codes = sb.tile([P, width], U32, name=name + "_codes", align_bytes=64)
+            plane = sb.tile([P, width], U8, name=name + "_plane", align_bytes=64)
+            nc.vector.quantize_mx(codes[:].bitcast(FP8X4), plane[:], grouped[:])
+            return codes, plane
+
+        def round_dealt(g, vector_share):
+            grouped = sb.tile([P, PACK * H], BF16, name="w_bf%d" % g, align_bytes=64)
+            dst = grouped[:].rearrange("p (t m j) -> p m j t", t=PACK, j=PACK)
+            src = w_raw[g][:].rearrange("p j (m t) -> p m j t", t=PACK)
+            if vector_share > 0:
+                nc.vector.tensor_copy(dst[:, :vector_share], src[:, :vector_share])
+            nc.scalar.copy(dst[:, vector_share:], src[:, vector_share:])
+            return grouped
+
+        def round_plain(raw, width, name, copy):
+            grouped = sb.tile([P, PACK * width], BF16, name=name + "_bf", align_bytes=64)
+            copy(grouped[:].rearrange("p (c i j) -> p c j i", i=4, j=PACK), raw[:].rearrange("p j (c i) -> p c j i", i=4))
+            return grouped
+
+        hidden = [ps.tile([P, PACK, CHUNK], F32, name="hidden%d" % c) for c in range(N_CHUNKS)]
+        shares = [32, 48, 64, 64, 84]
+        for g in range(4):
+            z, side = divmod(g, 2)
+            w_codes, w_plane = quantize(round_dealt(g, shares[g]), H, "w%d" % g)
+            for c in range(N_CHUNKS):
+                cols = slice(c * CHUNK, (c + 1) * CHUNK)
+                plane_cols = slice(side * V + c * CHUNK, side * V + (c + 1) * CHUNK)
+                for t in range(PACK):
+                    nc.tensor.matmul_mx(
+                        hidden[c][:, t, :],
+                        lhsT=w_codes[:, t * P : (t + 1) * P].bitcast(FP8X4),
+                        lhsT_scale=w_plane[:, t * P : (t + 1) * P],
+                        rhs=x_codes[z, side][:, cols].bitcast(FP8X4),
+                        rhs_scale=x_planes[4 * z :, plane_cols],
+                        start=(g == 0 and t == 0),
+                        stop=False,
+                    )
+        w3_codes, w3_plane = quantize(round_dealt(4, shares[4]), H, "w3")
+        e_q = []
+        for c in range(N_CHUNKS):
+            copy = nc.scalar.copy if c < 2 else nc.vector.tensor_copy
+            e_codes, e_plane = quantize(round_plain(e_raw[c], CHUNK, "e%d" % c, copy), CHUNK, "e%d" % c)
+            for t in range(PACK):
+                nc.tensor.matmul_mx(
+                    hidden[c][:, t, :],
+                    lhsT=w3_codes[:, t * P : (t + 1) * P].bitcast(FP8X4),
+                    lhsT_scale=w3_plane[:, t * P : (t + 1) * P],
+                    rhs=e_codes[:].bitcast(FP8X4),
+                    rhs_scale=e_plane[:],
+                    start=False,
+                    stop=(t == PACK - 1),
+                )
+        w4_codes, w4_plane = quantize(round_plain(w4_raw, N, "w4", nc.vector.tensor_copy), N, "w4")
+        for c in range(N_CHUNKS):
+            h_bf = sb.tile([P, CHUNK * PACK], BF16, name="h_bf%d" % c, align_bytes=64)
+            nc.scalar.activation(h_bf[:].rearrange("p (v t) -> p v t", t=PACK), hidden[c][:].rearrange("p t v -> p v t"), GELU, bias=gelu_bias[:])
+            h_codes, h_plane = quantize(h_bf, CHUNK, "h%d" % c)
+            result = ps.tile([N, CHUNK], F32, name="result%d" % c)
+            nc.tensor.matmul_mx(
+                result[:],
+                lhsT=w4_codes[:].bitcast(FP8X4),
+                lhsT_scale=w4_plane[:],
+                rhs=h_codes[:].bitcast(FP8X4),
+                rhs_scale=h_plane[:],
+                start=True,
+                stop=True,
+            )
+            staged = sb.tile([N, CHUNK], F32, name="staged%d" % c)
+            nc.vector.tensor_copy(staged[:], result[:])
+            nc.sync.dma_start(out[:, c * CHUNK : (c + 1) * CHUNK], staged[:])

@@ -40,9 +40,8 @@ def tile_picked_edgeup_gelu_p_kernel(tc, x_words, x_scales, eT, w1, w2, w3, w4, 
         word_tables = [sb.tile([P, T], I32, name="word_table%d" % z, align_bytes=64) for z in range(2)]
         nc.sync.dma_start(word_tables[0][:], x_words[0].rearrange("p n r -> p (n r)").bitcast(I32))
         for q in range(4):
-            nc.scalar.dma_start(scale_table[32 * q : 32 * q + 8, :].bitcast(I32), x_scales[:, 4 * q : 4 * q + 4, :].bitcast(I32))
+            nc.gpsimd.dma_start(scale_table[32 * q : 32 * q + 8, :].bitcast(I32), x_scales[:, 4 * q : 4 * q + 4, :].bitcast(I32))
         nc.scalar.activation(gelu_bias[:], zero[:], GELU)
-        nc.sync.dma_start(word_tables[1][:], x_words[1].rearrange("p n r -> p (n r)").bitcast(I32))
 
         first_rows = [w1[0:K_PASS, :], w2[0:K_PASS, :], w1[K_PASS:K, :], w2[K_PASS:K, :], w3]
         w_raw = []
@@ -50,11 +49,13 @@ def tile_picked_edgeup_gelu_p_kernel(tc, x_words, x_scales, eT, w1, w2, w3, w4, 
             raw = sb.tile([P, PACK, H], F32, name="w_raw%d" % g)
             nc.sync.dma_start(raw[:], rows.rearrange("(p j) c -> p j c", j=PACK))
             w_raw.append(raw)
+            if g == 0:
+                nc.sync.dma_start(word_tables[1][:], x_words[1].rearrange("p n r -> p (n r)").bitcast(I32))
         e_raw = []
-        for c in range(N_CHUNKS):
-            raw = sb.tile([P, PACK, CHUNK], F32, name="e_raw%d" % c)
-            nc.sync.dma_start(raw[:], eT[:, c * CHUNK : (c + 1) * CHUNK].rearrange("(p j) c -> p j c", j=PACK))
-            e_raw.append(raw)
+        for first, count in ((0, 2), (2, 1), (3, 1)):
+            raw = sb.tile([P, PACK, count * CHUNK], F32, name="e_raw%d" % first)
+            nc.sync.dma_start(raw[:], eT[:, first * CHUNK : (first + count) * CHUNK].rearrange("(p j) c -> p j c", j=PACK))
+            e_raw.extend(raw[:, :, i * CHUNK : (i + 1) * CHUNK] for i in range(count))
         w4_raw = sb.tile([P, PACK, N], F32, name="w4_raw")
         nc.sync.dma_start(w4_raw[:], w4.rearrange("(p j) c -> p j c", j=PACK))
 
@@ -88,11 +89,11 @@ def tile_picked_edgeup_gelu_p_kernel(tc, x_words, x_scales, eT, w1, w2, w3, w4, 
 
         def round_plain(raw, width, name, copy):
             grouped = sb.tile([P, PACK * width], BF16, name=name + "_bf", align_bytes=64)
-            copy(grouped[:].rearrange("p (c i j) -> p c j i", i=4, j=PACK), raw[:].rearrange("p j (c i) -> p c j i", i=4))
+            copy(grouped[:].rearrange("p (c i j) -> p c j i", i=4, j=PACK), raw.rearrange("p j (c i) -> p c j i", i=4))
             return grouped
 
         hidden = [ps.tile([P, PACK, CHUNK], F32, name="hidden%d" % c) for c in range(N_CHUNKS)]
-        shares = [32, 48, 64, 64, 84]
+        shares = [0, 32, 48, 64, 84]
         for g in range(4):
             z, side = divmod(g, 2)
             w_codes, w_plane = quantize(round_dealt(g, shares[g]), H, "w%d" % g)
@@ -112,7 +113,7 @@ def tile_picked_edgeup_gelu_p_kernel(tc, x_words, x_scales, eT, w1, w2, w3, w4, 
         w3_codes, w3_plane = quantize(round_dealt(4, shares[4]), H, "w3")
         e_q = []
         for c in range(N_CHUNKS):
-            copy = nc.scalar.copy if c < 2 else nc.vector.tensor_copy
+            copy = nc.scalar.copy if c % 2 == 0 else nc.vector.tensor_copy
             e_codes, e_plane = quantize(round_plain(e_raw[c], CHUNK, "e%d" % c, copy), CHUNK, "e%d" % c)
             for t in range(PACK):
                 nc.tensor.matmul_mx(
@@ -124,7 +125,7 @@ def tile_picked_edgeup_gelu_p_kernel(tc, x_words, x_scales, eT, w1, w2, w3, w4, 
                     start=False,
                     stop=(t == PACK - 1),
                 )
-        w4_codes, w4_plane = quantize(round_plain(w4_raw, N, "w4", nc.vector.tensor_copy), N, "w4")
+        w4_codes, w4_plane = quantize(round_plain(w4_raw[:], N, "w4", nc.vector.tensor_copy), N, "w4")
         for c in range(N_CHUNKS):
             h_bf = sb.tile([P, CHUNK * PACK], BF16, name="h_bf%d" % c, align_bytes=64)
             nc.scalar.activation(h_bf[:].rearrange("p (v t) -> p v t", t=PACK), hidden[c][:].rearrange("p t v -> p v t"), GELU, bias=gelu_bias[:])

@@ -17,51 +17,74 @@ GELU = mybir.ActivationFunctionType.Gelu_apprx_tanh
 P = 128
 PACK = 4
 K_PASS = P * PACK
+RUN = 4
+QUADRANT = 32
 CHUNK = 128
 N_CHUNKS = V // CHUNK
-OFFS_COLS = V // 16
+SIDE_COLS = V // 16
+
+VECTOR_SHARE = (0, 12, 12, 18)
+EDGE_LOADS = ((0, 1), (1, 2), (3, 1))
+SCALAR_EDGE_CHUNKS = 2
+W3_SCALAR_TILE = 3
+W4_BYTES = PACK * N * 4
 
 
 def tile_picked_edgeup_gelu_p_kernel(tc, x_words, x_scales, eT, w1, w2, w3, w4, offs, out):
     nc = tc.nc
     with ExitStack() as ctx:
         sb = ctx.enter_context(tc.tile_pool(name="sb", bufs=1))
+        shared = ctx.enter_context(tc.tile_pool(name="shared", bufs=1))
         ps = ctx.enter_context(tc.psum_pool(name="ps", bufs=1))
 
-        offsets = sb.tile([P, 2 * OFFS_COLS], U16, name="offsets")
-        nc.sync.dma_start(offsets[:], offs)
+        offsets = sb.tile([P, 2 * SIDE_COLS], U16, name="offsets")
 
-        scale_table = sb.tile([P, T], U8, name="scale_table", align_bytes=64)
+        scale_table = shared.tile([P, T], U8, name="scale_table", align_bytes=64, offset=W4_BYTES)
         nc.vector.memset(scale_table[:].bitcast(I32), 0)
         zero = sb.tile([P, 1], F32, name="zero")
         nc.vector.memset(zero[:], 0.0)
         gelu_bias = sb.tile([P, 1], F32, name="gelu_bias")
 
-        word_tables = [sb.tile([P, T], I32, name="word_table%d" % z, align_bytes=64) for z in range(2)]
-        nc.sync.dma_start(word_tables[0][:], x_words[0].rearrange("p n r -> p (n r)").bitcast(I32))
-        for q in range(4):
-            nc.gpsimd.dma_start(scale_table[32 * q : 32 * q + 8, :].bitcast(I32), x_scales[:, 4 * q : 4 * q + 4, :].bitcast(I32))
-        nc.scalar.activation(gelu_bias[:], zero[:], GELU)
-
-        first_rows = [w1[0:K_PASS, :], w2[0:K_PASS, :], w1[K_PASS:K, :], w2[K_PASS:K, :], w3]
-        w_raw = []
-        for g, rows in enumerate(first_rows):
-            raw = sb.tile([P, PACK, H], F32, name="w_raw%d" % g)
+        def load_rows(rows, name):
+            raw = sb.tile([P, PACK, rows.shape[1]], F32, name=name)
             nc.sync.dma_start(raw[:], rows.rearrange("(p j) c -> p j c", j=PACK))
-            w_raw.append(raw)
-            if g == 0:
-                nc.sync.dma_start(word_tables[1][:], x_words[1].rearrange("p n r -> p (n r)").bitcast(I32))
+            return raw
+
+        def load_words(z):
+            table = sb.tile([P, T], I32, name="word_table%d" % z, align_bytes=64)
+            nc.sync.dma_start(table[:], x_words[z].rearrange("p n r -> p (n r)").bitcast(I32))
+            return table
+
+        def load_scales(z):
+            for q in range(P // QUADRANT):
+                first = QUADRANT * q + PACK * z
+                rows = x_scales[z, PACK * q : PACK * (q + 1), :]
+                nc.sync.dma_start(scale_table[first : first + PACK, :].bitcast(I32), rows.bitcast(I32))
+
+        word_tables = [load_words(0)]
+        nc.sync.dma_start(offsets[:], offs)
+        load_scales(0)
+        nc.scalar.activation(gelu_bias[:], zero[:], GELU)
+        w_raw = [load_rows(w1[0:K_PASS, :], "w_raw0")]
+        load_scales(1)
+        w_raw.append(load_rows(w2[0:K_PASS, :], "w_raw1"))
+        word_tables.append(load_words(1))
+        w_raw.append(load_rows(w1[K_PASS:K, :], "w_raw2"))
+        w_raw.append(load_rows(w2[K_PASS:K, :], "w_raw3"))
+        w3_raw = load_rows(w3, "w3_raw")
         e_raw = []
-        for first, count in ((0, 2), (2, 1), (3, 1)):
-            raw = sb.tile([P, PACK, count * CHUNK], F32, name="e_raw%d" % first)
-            nc.sync.dma_start(raw[:], eT[:, first * CHUNK : (first + count) * CHUNK].rearrange("(p j) c -> p j c", j=PACK))
+        for first, count in EDGE_LOADS:
+            raw = load_rows(eT[:, first * CHUNK : (first + count) * CHUNK], "e_raw%d" % first)
             e_raw.extend(raw[:, :, i * CHUNK : (i + 1) * CHUNK] for i in range(count))
-        w4_raw = sb.tile([P, PACK, N], F32, name="w4_raw")
-        nc.sync.dma_start(w4_raw[:], w4.rearrange("(p j) c -> p j c", j=PACK))
+        w4_raw = shared.tile([P, PACK, N], F32, name="w4_raw", align_bytes=64, offset=0)
+        w4_dealt = w4.rearrange("(u t e) n -> e u t n", t=PACK, e=RUN)
+        for e in range(RUN):
+            nc.sync.dma_start(w4_raw[e:P:RUN, :, :], w4_dealt[e])
 
         def gather_words(z, side):
             picked = sb.tile([P, V], U32, name="x_codes%d%d" % (z, side), align_bytes=64)
-            nc.vector.tensor_copy(picked[:], word_tables[z][:].bitcast(U32).indirect(offsets[:, side * OFFS_COLS : (side + 1) * OFFS_COLS]))
+            entries = offsets[:, side * SIDE_COLS : (side + 1) * SIDE_COLS]
+            nc.vector.tensor_copy(picked[:], word_tables[z][:].bitcast(U32).indirect(entries))
             return picked
 
         x_codes = {}
@@ -72,31 +95,42 @@ def tile_picked_edgeup_gelu_p_kernel(tc, x_words, x_scales, eT, w1, w2, w3, w4, 
         x_codes[1, 0] = gather_words(1, 0)
         x_codes[1, 1] = gather_words(1, 1)
 
-        def quantize(grouped, width, name):
-            codes = sb.tile([P, width], U32, name=name + "_codes", align_bytes=64)
-            plane = sb.tile([P, width], U8, name=name + "_plane", align_bytes=64)
+        def codes_tile(width, name):
+            return sb.tile([P, width], U32, name=name + "_codes", align_bytes=64)
+
+        def plane_tile(width, name):
+            return sb.tile([P, width], U8, name=name + "_plane", align_bytes=64)
+
+        def quantize(grouped, codes, plane):
             nc.vector.quantize_mx(codes[:].bitcast(FP8X4), plane[:], grouped[:])
             return codes, plane
 
-        def round_dealt(g, vector_share):
+        def round_dealt(g):
             grouped = sb.tile([P, PACK * H], BF16, name="w_bf%d" % g, align_bytes=64)
-            dst = grouped[:].rearrange("p (t m j) -> p m j t", t=PACK, j=PACK)
-            src = w_raw[g][:].rearrange("p j (m t) -> p m j t", t=PACK)
-            if vector_share > 0:
-                nc.vector.tensor_copy(dst[:, :vector_share], src[:, :vector_share])
-            nc.scalar.copy(dst[:, vector_share:], src[:, vector_share:])
+            dst = grouped[:].rearrange("p (t u e j) -> p u t j e", t=PACK, e=RUN, j=PACK)
+            src = w_raw[g][:].rearrange("p j (u t e) -> p u t j e", t=PACK, e=RUN)
+            share = VECTOR_SHARE[g]
+            if share > 0:
+                nc.vector.tensor_copy(dst[:, :share], src[:, :share])
+            nc.scalar.copy(dst[:, share:], src[:, share:])
             return grouped
 
         def round_plain(raw, width, name, copy):
             grouped = sb.tile([P, PACK * width], BF16, name=name + "_bf", align_bytes=64)
-            copy(grouped[:].rearrange("p (c i j) -> p c j i", i=4, j=PACK), raw.rearrange("p j (c i) -> p c j i", i=4))
+            dst = grouped[:].rearrange("p (c e j) -> p c j e", e=RUN, j=PACK)
+            copy(dst, raw.rearrange("p j (c e) -> p c j e", e=RUN))
             return grouped
 
         hidden = [ps.tile([P, PACK, CHUNK], F32, name="hidden%d" % c) for c in range(N_CHUNKS)]
-        shares = [0, 32, 48, 64, 84]
         for g in range(4):
             z, side = divmod(g, 2)
-            w_codes, w_plane = quantize(round_dealt(g, shares[g]), H, "w%d" % g)
+            grouped = round_dealt(g)
+            codes = codes_tile(H, "w%d" % g)
+            if g == 0:
+                plane = shared.tile([P, H], U8, name="w0_plane", align_bytes=64, offset=W4_BYTES)
+            else:
+                plane = plane_tile(H, "w%d" % g)
+            w_codes, w_plane = quantize(grouped, codes, plane)
             for c in range(N_CHUNKS):
                 cols = slice(c * CHUNK, (c + 1) * CHUNK)
                 plane_cols = slice(side * V + c * CHUNK, side * V + (c + 1) * CHUNK)
@@ -106,30 +140,48 @@ def tile_picked_edgeup_gelu_p_kernel(tc, x_words, x_scales, eT, w1, w2, w3, w4, 
                         lhsT=w_codes[:, t * P : (t + 1) * P].bitcast(FP8X4),
                         lhsT_scale=w_plane[:, t * P : (t + 1) * P],
                         rhs=x_codes[z, side][:, cols].bitcast(FP8X4),
-                        rhs_scale=x_planes[4 * z :, plane_cols],
+                        rhs_scale=x_planes[PACK * z :, plane_cols],
                         start=(g == 0 and t == 0),
                         stop=False,
                     )
-        w3_codes, w3_plane = quantize(round_dealt(4, shares[4]), H, "w3")
-        e_q = []
+
+        w3_src = w3_raw[:].rearrange("p j (u t e) -> p t u j e", t=PACK, e=RUN)
+        w3_bf = []
+        for t in range(PACK):
+            grouped = sb.tile([P, PACK * P], BF16, name="w3_bf%d" % t, align_bytes=64)
+            copy = nc.scalar.copy if t == W3_SCALAR_TILE else nc.vector.tensor_copy
+            copy(grouped[:].rearrange("p (u e j) -> p u j e", e=RUN, j=PACK), w3_src[:, t])
+            w3_bf.append(grouped)
+        w3_mx = [quantize(w3_bf[t], codes_tile(P, "w3t%d" % t), plane_tile(P, "w3t%d" % t)) for t in range(PACK)]
+
         for c in range(N_CHUNKS):
-            copy = nc.scalar.copy if c % 2 == 0 else nc.vector.tensor_copy
-            e_codes, e_plane = quantize(round_plain(e_raw[c], CHUNK, "e%d" % c, copy), CHUNK, "e%d" % c)
+            copy = nc.scalar.copy if c < SCALAR_EDGE_CHUNKS else nc.vector.tensor_copy
+            grouped = round_plain(e_raw[c], CHUNK, "e%d" % c, copy)
+            e_codes, e_plane = quantize(grouped, codes_tile(CHUNK, "e%d" % c), plane_tile(CHUNK, "e%d" % c))
             for t in range(PACK):
+                w3_codes, w3_plane = w3_mx[t]
                 nc.tensor.matmul_mx(
                     hidden[c][:, t, :],
-                    lhsT=w3_codes[:, t * P : (t + 1) * P].bitcast(FP8X4),
-                    lhsT_scale=w3_plane[:, t * P : (t + 1) * P],
+                    lhsT=w3_codes[:].bitcast(FP8X4),
+                    lhsT_scale=w3_plane[:],
                     rhs=e_codes[:].bitcast(FP8X4),
                     rhs_scale=e_plane[:],
                     start=False,
                     stop=(t == PACK - 1),
                 )
-        w4_codes, w4_plane = quantize(round_plain(w4_raw[:], N, "w4", nc.vector.tensor_copy), N, "w4")
+
+        grouped = round_plain(w4_raw[:], N, "w4", nc.vector.tensor_copy)
+        w4_codes, w4_plane = quantize(grouped, codes_tile(N, "w4"), plane_tile(N, "w4"))
         for c in range(N_CHUNKS):
             h_bf = sb.tile([P, CHUNK * PACK], BF16, name="h_bf%d" % c, align_bytes=64)
-            nc.scalar.activation(h_bf[:].rearrange("p (v t) -> p v t", t=PACK), hidden[c][:].rearrange("p t v -> p v t"), GELU, bias=gelu_bias[:])
-            h_codes, h_plane = quantize(h_bf, CHUNK, "h%d" % c)
+            nc.scalar.activation(
+                h_bf[:].rearrange("p (v t) -> p v t", t=PACK),
+                hidden[c][:].rearrange("p t v -> p v t"),
+                GELU,
+                bias=gelu_bias[:],
+            )
+            codes = shared.tile([P, CHUNK], U32, name="h_codes%d" % c, align_bytes=64, offset=4 * CHUNK * c)
+            h_codes, h_plane = quantize(h_bf, codes, plane_tile(CHUNK, "h%d" % c))
             result = ps.tile([N, CHUNK], F32, name="result%d" % c)
             nc.tensor.matmul_mx(
                 result[:],

@@ -22,11 +22,12 @@ QUADRANT = 32
 CHUNK = 128
 N_CHUNKS = V // CHUNK
 SIDE_COLS = V // 16
+HALF = P // 2
 
-VECTOR_SHARE = (0, 12, 12, 18)
-EDGE_LOADS = ((0, 1), (1, 2), (3, 1))
-SCALAR_EDGE_CHUNKS = 2
-W3_SCALAR_TILE = 3
+VECTOR_SHARE = (0, 32, 64, 80)
+W3_VECTOR_SHARE = (24, 24)
+EDGE_LOADS = ((0, 1), (1, 1), (2, 1), (3, 1))
+SCALAR_EDGE_CHUNKS = (1, 2,)
 W4_BYTES = PACK * N * 4
 
 
@@ -45,8 +46,9 @@ def tile_picked_edgeup_gelu_p_kernel(tc, x_words, x_scales, eT, w1, w2, w3, w4, 
         nc.vector.memset(zero[:], 0.0)
         gelu_bias = sb.tile([P, 1], F32, name="gelu_bias")
 
-        def load_rows(rows, name):
-            raw = sb.tile([P, PACK, rows.shape[1]], F32, name=name)
+        def load_rows(rows, name, raw=None):
+            if raw is None:
+                raw = sb.tile([P, PACK, rows.shape[1]], F32, name=name)
             nc.sync.dma_start(raw[:], rows.rearrange("(p j) c -> p j c", j=PACK))
             return raw
 
@@ -55,31 +57,25 @@ def tile_picked_edgeup_gelu_p_kernel(tc, x_words, x_scales, eT, w1, w2, w3, w4, 
             nc.sync.dma_start(table[:], x_words[z].rearrange("p n r -> p (n r)").bitcast(I32))
             return table
 
-        def load_scales(z):
-            for q in range(P // QUADRANT):
-                first = QUADRANT * q + PACK * z
-                rows = x_scales[z, PACK * q : PACK * (q + 1), :]
-                nc.sync.dma_start(scale_table[first : first + PACK, :].bitcast(I32), rows.bitcast(I32))
-
         word_tables = [load_words(0)]
         nc.sync.dma_start(offsets[:], offs)
-        load_scales(0)
+        for q in range(P // QUADRANT):
+            rows = x_scales[:, PACK * q : PACK * (q + 1), :]
+            first = QUADRANT * q
+            nc.sync.dma_start(scale_table[first : first + 2 * PACK, :].bitcast(I32), rows.bitcast(I32))
         nc.scalar.activation(gelu_bias[:], zero[:], GELU)
         w_raw = [load_rows(w1[0:K_PASS, :], "w_raw0")]
-        load_scales(1)
-        w_raw.append(load_rows(w2[0:K_PASS, :], "w_raw1"))
         word_tables.append(load_words(1))
+        w_raw.append(load_rows(w2[0:K_PASS, :], "w_raw1"))
         w_raw.append(load_rows(w1[K_PASS:K, :], "w_raw2"))
         w_raw.append(load_rows(w2[K_PASS:K, :], "w_raw3"))
-        w3_raw = load_rows(w3, "w3_raw")
+        w3_raw = [load_rows(w3[:, a * H // 2 : (a + 1) * H // 2], "w3_raw%d" % a) for a in range(2)]
         e_raw = []
         for first, count in EDGE_LOADS:
             raw = load_rows(eT[:, first * CHUNK : (first + count) * CHUNK], "e_raw%d" % first)
             e_raw.extend(raw[:, :, i * CHUNK : (i + 1) * CHUNK] for i in range(count))
         w4_raw = shared.tile([P, PACK, N], F32, name="w4_raw", align_bytes=64, offset=0)
-        w4_dealt = w4.rearrange("(u t e) n -> e u t n", t=PACK, e=RUN)
-        for e in range(RUN):
-            nc.sync.dma_start(w4_raw[e:P:RUN, :, :], w4_dealt[e])
+        load_rows(w4, "w4_raw", w4_raw)
 
         def gather_words(z, side):
             picked = sb.tile([P, V], U32, name="x_codes%d%d" % (z, side), align_bytes=64)
@@ -102,17 +98,17 @@ def tile_picked_edgeup_gelu_p_kernel(tc, x_words, x_scales, eT, w1, w2, w3, w4, 
             return sb.tile([P, width], U8, name=name + "_plane", align_bytes=64)
 
         def quantize(grouped, codes, plane):
-            nc.vector.quantize_mx(codes[:].bitcast(FP8X4), plane[:], grouped[:])
-            return codes, plane
+            nc.vector.quantize_mx(codes.bitcast(FP8X4), plane, grouped)
 
-        def round_dealt(g):
-            grouped = sb.tile([P, PACK * H], BF16, name="w_bf%d" % g, align_bytes=64)
-            dst = grouped[:].rearrange("p (t u e j) -> p u t j e", t=PACK, e=RUN, j=PACK)
-            src = w_raw[g][:].rearrange("p j (u t e) -> p u t j e", t=PACK, e=RUN)
-            share = VECTOR_SHARE[g]
+        def round_dealt(raw, share, name):
+            width = raw.shape[2] // PACK
+            grouped = sb.tile([P, PACK, width * PACK], BF16, name=name, align_bytes=64)
+            dst = grouped[:].rearrange("p t (m j) -> p m j t", j=PACK)
+            src = raw[:].rearrange("p j (m t) -> p m j t", t=PACK)
             if share > 0:
                 nc.vector.tensor_copy(dst[:, :share], src[:, :share])
-            nc.scalar.copy(dst[:, share:], src[:, share:])
+            if share < width:
+                nc.scalar.copy(dst[:, share:], src[:, share:])
             return grouped
 
         def round_plain(raw, width, name, copy):
@@ -124,13 +120,13 @@ def tile_picked_edgeup_gelu_p_kernel(tc, x_words, x_scales, eT, w1, w2, w3, w4, 
         hidden = [ps.tile([P, PACK, CHUNK], F32, name="hidden%d" % c) for c in range(N_CHUNKS)]
         for g in range(4):
             z, side = divmod(g, 2)
-            grouped = round_dealt(g)
-            codes = codes_tile(H, "w%d" % g)
+            grouped = round_dealt(w_raw[g], VECTOR_SHARE[g], "w_bf%d" % g)
+            w_codes = codes_tile(H, "w%d" % g)
             if g == 0:
-                plane = shared.tile([P, H], U8, name="w0_plane", align_bytes=64, offset=W4_BYTES)
+                w_plane = shared.tile([P, H], U8, name="w0_plane", align_bytes=64, offset=W4_BYTES)
             else:
-                plane = plane_tile(H, "w%d" % g)
-            w_codes, w_plane = quantize(grouped, codes, plane)
+                w_plane = plane_tile(H, "w%d" % g)
+            quantize(grouped[:].rearrange("p t c -> p (t c)"), w_codes[:], w_plane[:])
             for c in range(N_CHUNKS):
                 cols = slice(c * CHUNK, (c + 1) * CHUNK)
                 plane_cols = slice(side * V + c * CHUNK, side * V + (c + 1) * CHUNK)
@@ -145,25 +141,33 @@ def tile_picked_edgeup_gelu_p_kernel(tc, x_words, x_scales, eT, w1, w2, w3, w4, 
                         stop=False,
                     )
 
-        w3_src = w3_raw[:].rearrange("p j (u t e) -> p t u j e", t=PACK, e=RUN)
-        w3_bf = []
-        for t in range(PACK):
-            grouped = sb.tile([P, PACK * P], BF16, name="w3_bf%d" % t, align_bytes=64)
-            copy = nc.scalar.copy if t == W3_SCALAR_TILE else nc.vector.tensor_copy
-            copy(grouped[:].rearrange("p (u e j) -> p u j e", e=RUN, j=PACK), w3_src[:, t])
-            w3_bf.append(grouped)
-        w3_mx = [quantize(w3_bf[t], codes_tile(P, "w3t%d" % t), plane_tile(P, "w3t%d" % t)) for t in range(PACK)]
+        w3_codes = [codes_tile(P, "w3t%d" % t) for t in range(PACK)]
+        w3_planes = [plane_tile(P, "w3t%d" % t) for t in range(PACK)]
+        e_bf = {}
+
+        def round_edges(c):
+            copy = nc.scalar.copy if c in SCALAR_EDGE_CHUNKS else nc.vector.tensor_copy
+            e_bf[c] = round_plain(e_raw[c], CHUNK, "e%d" % c, copy)
+
+        for a in range(2):
+            grouped = round_dealt(w3_raw[a], W3_VECTOR_SHARE[a], "w3_bf%d" % a)
+            if a == 1:
+                round_edges(0)
+            places = slice(a * HALF, (a + 1) * HALF)
+            for t in range(PACK):
+                quantize(grouped[:, t, :], w3_codes[t][:, places], w3_planes[t][:, places])
 
         for c in range(N_CHUNKS):
-            copy = nc.scalar.copy if c < SCALAR_EDGE_CHUNKS else nc.vector.tensor_copy
-            grouped = round_plain(e_raw[c], CHUNK, "e%d" % c, copy)
-            e_codes, e_plane = quantize(grouped, codes_tile(CHUNK, "e%d" % c), plane_tile(CHUNK, "e%d" % c))
+            if c + 1 < N_CHUNKS:
+                round_edges(c + 1)
+            grouped = e_bf[c]
+            e_codes, e_plane = codes_tile(CHUNK, "e%d" % c), plane_tile(CHUNK, "e%d" % c)
+            quantize(grouped[:], e_codes[:], e_plane[:])
             for t in range(PACK):
-                w3_codes, w3_plane = w3_mx[t]
                 nc.tensor.matmul_mx(
                     hidden[c][:, t, :],
-                    lhsT=w3_codes[:].bitcast(FP8X4),
-                    lhsT_scale=w3_plane[:],
+                    lhsT=w3_codes[t][:].bitcast(FP8X4),
+                    lhsT_scale=w3_planes[t][:],
                     rhs=e_codes[:].bitcast(FP8X4),
                     rhs_scale=e_plane[:],
                     start=False,
@@ -171,7 +175,8 @@ def tile_picked_edgeup_gelu_p_kernel(tc, x_words, x_scales, eT, w1, w2, w3, w4, 
                 )
 
         grouped = round_plain(w4_raw[:], N, "w4", nc.vector.tensor_copy)
-        w4_codes, w4_plane = quantize(grouped, codes_tile(N, "w4"), plane_tile(N, "w4"))
+        w4_codes, w4_plane = codes_tile(N, "w4"), plane_tile(N, "w4")
+        quantize(grouped[:], w4_codes[:], w4_plane[:])
         for c in range(N_CHUNKS):
             h_bf = sb.tile([P, CHUNK * PACK], BF16, name="h_bf%d" % c, align_bytes=64)
             nc.scalar.activation(
@@ -180,8 +185,8 @@ def tile_picked_edgeup_gelu_p_kernel(tc, x_words, x_scales, eT, w1, w2, w3, w4, 
                 GELU,
                 bias=gelu_bias[:],
             )
-            codes = shared.tile([P, CHUNK], U32, name="h_codes%d" % c, align_bytes=64, offset=4 * CHUNK * c)
-            h_codes, h_plane = quantize(h_bf, codes, plane_tile(CHUNK, "h%d" % c))
+            h_codes, h_plane = codes_tile(CHUNK, "h%d" % c), plane_tile(CHUNK, "h%d" % c)
+            quantize(h_bf[:], h_codes[:], h_plane[:])
             result = ps.tile([N, CHUNK], F32, name="result%d" % c)
             nc.tensor.matmul_mx(
                 result[:],

@@ -22,12 +22,11 @@ QUADRANT = 32
 CHUNK = 128
 N_CHUNKS = V // CHUNK
 SIDE_COLS = V // 16
-HALF = P // 2
 
 VECTOR_SHARE = (0, 32, 64, 80)
-W3_VECTOR_SHARE = (24, 24)
-EDGE_LOADS = ((0, 1), (1, 1), (2, 1), (3, 1))
-SCALAR_EDGE_CHUNKS = (1, 2,)
+W3_VECTOR_SHARE = 80
+EDGE_LOADS = ((0, 1), (1, 2), (3, 1))
+SCALAR_EDGE_CHUNKS = (2,)
 W4_BYTES = PACK * N * 4
 
 
@@ -57,19 +56,22 @@ def tile_picked_edgeup_gelu_p_kernel(tc, x_words, x_scales, eT, w1, w2, w3, w4, 
             nc.sync.dma_start(table[:], x_words[z].rearrange("p n r -> p (n r)").bitcast(I32))
             return table
 
+        def load_scales(z):
+            for r in range(PACK):
+                rows = x_scales[z, r :: PACK, :]
+                nc.sync.dma_start(scale_table[PACK * z + r :: QUADRANT, :].bitcast(I32), rows.bitcast(I32))
+
         word_tables = [load_words(0)]
         nc.sync.dma_start(offsets[:], offs)
-        for q in range(P // QUADRANT):
-            rows = x_scales[:, PACK * q : PACK * (q + 1), :]
-            first = QUADRANT * q
-            nc.sync.dma_start(scale_table[first : first + 2 * PACK, :].bitcast(I32), rows.bitcast(I32))
+        load_scales(0)
         nc.scalar.activation(gelu_bias[:], zero[:], GELU)
         w_raw = [load_rows(w1[0:K_PASS, :], "w_raw0")]
+        load_scales(1)
         word_tables.append(load_words(1))
         w_raw.append(load_rows(w2[0:K_PASS, :], "w_raw1"))
         w_raw.append(load_rows(w1[K_PASS:K, :], "w_raw2"))
         w_raw.append(load_rows(w2[K_PASS:K, :], "w_raw3"))
-        w3_raw = [load_rows(w3[:, a * H // 2 : (a + 1) * H // 2], "w3_raw%d" % a) for a in range(2)]
+        w3_raw = load_rows(w3, "w3_raw")
         e_raw = []
         for first, count in EDGE_LOADS:
             raw = load_rows(eT[:, first * CHUNK : (first + count) * CHUNK], "e_raw%d" % first)
@@ -149,20 +151,25 @@ def tile_picked_edgeup_gelu_p_kernel(tc, x_words, x_scales, eT, w1, w2, w3, w4, 
             copy = nc.scalar.copy if c in SCALAR_EDGE_CHUNKS else nc.vector.tensor_copy
             e_bf[c] = round_plain(e_raw[c], CHUNK, "e%d" % c, copy)
 
-        for a in range(2):
-            grouped = round_dealt(w3_raw[a], W3_VECTOR_SHARE[a], "w3_bf%d" % a)
-            if a == 1:
-                round_edges(0)
-            places = slice(a * HALF, (a + 1) * HALF)
-            for t in range(PACK):
-                quantize(grouped[:, t, :], w3_codes[t][:, places], w3_planes[t][:, places])
+        e_mx = {}
+
+        def quantize_edges(c):
+            e_mx[c] = codes_tile(CHUNK, "e%d" % c), plane_tile(CHUNK, "e%d" % c)
+            quantize(e_bf[c][:], e_mx[c][0][:], e_mx[c][1][:])
+
+        grouped = round_dealt(w3_raw, W3_VECTOR_SHARE, "w3_bf")
+        round_edges(0)
+        for t in range(PACK):
+            quantize(grouped[:, t, :], w3_codes[t][:], w3_planes[t][:])
+            if t == 0:
+                quantize_edges(0)
 
         for c in range(N_CHUNKS):
             if c + 1 < N_CHUNKS:
                 round_edges(c + 1)
-            grouped = e_bf[c]
-            e_codes, e_plane = codes_tile(CHUNK, "e%d" % c), plane_tile(CHUNK, "e%d" % c)
-            quantize(grouped[:], e_codes[:], e_plane[:])
+            if c > 0:
+                quantize_edges(c)
+            e_codes, e_plane = e_mx[c]
             for t in range(PACK):
                 nc.tensor.matmul_mx(
                     hidden[c][:, t, :],

@@ -25,8 +25,9 @@ SIDE_COLS = V // 16
 
 VECTOR_SHARE = (0, 32, 64, 80)
 W3_VECTOR_SHARE = 80
-EDGE_LOADS = ((0, 1), (1, 2), (3, 1))
-SCALAR_EDGE_CHUNKS = (2,)
+EDGE_LOADS = ((0, 2), (2, 2))
+SCALAR_EDGE_CHUNKS = (0, 1, 3,)
+SCALAR_RESULT_CHUNKS = (2,)
 W4_BYTES = PACK * N * 4
 
 
@@ -56,10 +57,11 @@ def tile_picked_edgeup_gelu_p_kernel(tc, x_words, x_scales, eT, w1, w2, w3, w4, 
             nc.sync.dma_start(table[:], x_words[z].rearrange("p n r -> p (n r)").bitcast(I32))
             return table
 
-        def load_scales(z):
-            for r in range(PACK):
-                rows = x_scales[z, r :: PACK, :]
-                nc.sync.dma_start(scale_table[PACK * z + r :: QUADRANT, :].bitcast(I32), rows.bitcast(I32))
+        def load_scales(run):
+            for r in range(2 * run, 2 * run + 2):
+                for z in range(2):
+                    rows = x_scales[z, r :: PACK, :]
+                    nc.sync.dma_start(scale_table[PACK * z + r :: QUADRANT, :].bitcast(I32), rows.bitcast(I32))
 
         word_tables = [load_words(0)]
         nc.sync.dma_start(offsets[:], offs)
@@ -161,8 +163,7 @@ def tile_picked_edgeup_gelu_p_kernel(tc, x_words, x_scales, eT, w1, w2, w3, w4, 
         round_edges(0)
         for t in range(PACK):
             quantize(grouped[:, t, :], w3_codes[t][:], w3_planes[t][:])
-            if t == 0:
-                quantize_edges(0)
+        quantize_edges(0)
 
         for c in range(N_CHUNKS):
             if c + 1 < N_CHUNKS:
@@ -205,5 +206,6 @@ def tile_picked_edgeup_gelu_p_kernel(tc, x_words, x_scales, eT, w1, w2, w3, w4, 
                 stop=True,
             )
             staged = sb.tile([N, CHUNK], F32, name="staged%d" % c)
-            nc.vector.tensor_copy(staged[:], result[:])
+            copy = nc.scalar.copy if c in SCALAR_RESULT_CHUNKS else nc.vector.tensor_copy
+            copy(staged[:], result[:])
             nc.sync.dma_start(out[:, c * CHUNK : (c + 1) * CHUNK], staged[:])

@@ -20,15 +20,15 @@ K_PASS = P * PACK
 RUN = 4
 QUADRANT = 32
 CHUNK = 128
+HALF = CHUNK // 2
 N_CHUNKS = V // CHUNK
+LAST = N_CHUNKS - 1
 SIDE_COLS = V // 16
 
 VECTOR_SHARE = (0, 32, 64, 80)
-W3_VECTOR_SHARE = 80
-EDGE_LOADS = ((0, 2), (2, 2))
-SCALAR_EDGE_CHUNKS = (0, 1, 3,)
-SCALAR_RESULT_CHUNKS = (2,)
-W4_BYTES = PACK * N * 4
+W3_VECTOR_SHARE = 84
+FIRST_CHUNK_VECTOR = 96
+EDGE_LOADS = ((0, 2), (2, 1), (3, 1))
 
 
 def tile_picked_edgeup_gelu_p_kernel(tc, x_words, x_scales, eT, w1, w2, w3, w4, offs, out):
@@ -40,15 +40,14 @@ def tile_picked_edgeup_gelu_p_kernel(tc, x_words, x_scales, eT, w1, w2, w3, w4, 
 
         offsets = sb.tile([P, 2 * SIDE_COLS], U16, name="offsets")
 
-        scale_table = shared.tile([P, T], U8, name="scale_table", align_bytes=64, offset=W4_BYTES)
+        scale_table = shared.tile([P, T], U8, name="scale_table", align_bytes=64, offset=0)
         nc.vector.memset(scale_table[:].bitcast(I32), 0)
         zero = sb.tile([P, 1], F32, name="zero")
         nc.vector.memset(zero[:], 0.0)
         gelu_bias = sb.tile([P, 1], F32, name="gelu_bias")
 
-        def load_rows(rows, name, raw=None):
-            if raw is None:
-                raw = sb.tile([P, PACK, rows.shape[1]], F32, name=name)
+        def load_rows(rows, name):
+            raw = sb.tile([P, PACK, rows.shape[1]], F32, name=name)
             nc.sync.dma_start(raw[:], rows.rearrange("(p j) c -> p j c", j=PACK))
             return raw
 
@@ -60,7 +59,7 @@ def tile_picked_edgeup_gelu_p_kernel(tc, x_words, x_scales, eT, w1, w2, w3, w4, 
         def load_scales(run):
             for r in range(2 * run, 2 * run + 2):
                 for z in range(2):
-                    rows = x_scales[z, r :: PACK, :]
+                    rows = x_scales[z, r::PACK, :]
                     nc.sync.dma_start(scale_table[PACK * z + r :: QUADRANT, :].bitcast(I32), rows.bitcast(I32))
 
         word_tables = [load_words(0)]
@@ -78,8 +77,7 @@ def tile_picked_edgeup_gelu_p_kernel(tc, x_words, x_scales, eT, w1, w2, w3, w4, 
         for first, count in EDGE_LOADS:
             raw = load_rows(eT[:, first * CHUNK : (first + count) * CHUNK], "e_raw%d" % first)
             e_raw.extend(raw[:, :, i * CHUNK : (i + 1) * CHUNK] for i in range(count))
-        w4_raw = shared.tile([P, PACK, N], F32, name="w4_raw", align_bytes=64, offset=0)
-        load_rows(w4, "w4_raw", w4_raw)
+        w4_raw = load_rows(w4, "w4_raw")
 
         def gather_words(z, side):
             picked = sb.tile([P, V], U32, name="x_codes%d%d" % (z, side), align_bytes=64)
@@ -95,117 +93,130 @@ def tile_picked_edgeup_gelu_p_kernel(tc, x_words, x_scales, eT, w1, w2, w3, w4, 
         x_codes[1, 0] = gather_words(1, 0)
         x_codes[1, 1] = gather_words(1, 1)
 
-        def codes_tile(width, name):
-            return sb.tile([P, width], U32, name=name + "_codes", align_bytes=64)
+        def mx_tiles(width, name):
+            codes = sb.tile([P, width], U32, name=name + "_codes", align_bytes=64)
+            plane = sb.tile([P, width], U8, name=name + "_plane", align_bytes=64)
+            return codes, plane
 
-        def plane_tile(width, name):
-            return sb.tile([P, width], U8, name=name + "_plane", align_bytes=64)
+        def quantize(grouped, mx, cols):
+            values = grouped[:, PACK * cols.start : PACK * cols.stop]
+            nc.vector.quantize_mx(mx[0][:, cols].bitcast(FP8X4), mx[1][:, cols], values)
 
-        def quantize(grouped, codes, plane):
-            nc.vector.quantize_mx(codes.bitcast(FP8X4), plane, grouped)
+        def multiply(result, weights, w_cols, codes, plane, start, stop):
+            nc.tensor.matmul_mx(
+                result,
+                lhsT=weights[0][:, w_cols].bitcast(FP8X4),
+                lhsT_scale=weights[1][:, w_cols],
+                rhs=codes.bitcast(FP8X4),
+                rhs_scale=plane,
+                start=start,
+                stop=stop,
+            )
 
         def round_dealt(raw, share, name):
-            width = raw.shape[2] // PACK
-            grouped = sb.tile([P, PACK, width * PACK], BF16, name=name, align_bytes=64)
-            dst = grouped[:].rearrange("p t (m j) -> p m j t", j=PACK)
+            grouped = sb.tile([P, PACK * H], BF16, name=name, align_bytes=64)
+            dst = grouped[:].rearrange("p (t m j) -> p m j t", t=PACK, j=PACK)
             src = raw[:].rearrange("p j (m t) -> p m j t", t=PACK)
             if share > 0:
                 nc.vector.tensor_copy(dst[:, :share], src[:, :share])
-            if share < width:
-                nc.scalar.copy(dst[:, share:], src[:, share:])
+            nc.scalar.copy(dst[:, share:], src[:, share:])
             return grouped
 
-        def round_plain(raw, width, name, copy):
-            grouped = sb.tile([P, PACK * width], BF16, name=name + "_bf", align_bytes=64)
-            dst = grouped[:].rearrange("p (c e j) -> p c j e", e=RUN, j=PACK)
-            copy(dst, raw.rearrange("p j (c e) -> p c j e", e=RUN))
-            return grouped
+        def round_plain(raw, grouped, cols, copy):
+            dst = grouped[:, PACK * cols.start : PACK * cols.stop].rearrange("p (c e j) -> p c j e", e=RUN, j=PACK)
+            copy(dst, raw[:, :, cols].rearrange("p j (c e) -> p c j e", e=RUN))
+
+        tile_cols = [slice(t * P, (t + 1) * P) for t in range(PACK)]
+        whole, low, high = slice(0, CHUNK), slice(0, HALF), slice(HALF, CHUNK)
 
         hidden = [ps.tile([P, PACK, CHUNK], F32, name="hidden%d" % c) for c in range(N_CHUNKS)]
         for g in range(4):
             z, side = divmod(g, 2)
             grouped = round_dealt(w_raw[g], VECTOR_SHARE[g], "w_bf%d" % g)
-            w_codes = codes_tile(H, "w%d" % g)
             if g == 0:
-                w_plane = shared.tile([P, H], U8, name="w0_plane", align_bytes=64, offset=W4_BYTES)
+                codes = sb.tile([P, H], U32, name="w0_codes", align_bytes=64)
+                w_mx = codes, shared.tile([P, H], U8, name="w0_plane", align_bytes=64, offset=0)
             else:
-                w_plane = plane_tile(H, "w%d" % g)
-            quantize(grouped[:].rearrange("p t c -> p (t c)"), w_codes[:], w_plane[:])
+                w_mx = mx_tiles(H, "w%d" % g)
+            quantize(grouped, w_mx, slice(0, H))
             for c in range(N_CHUNKS):
-                cols = slice(c * CHUNK, (c + 1) * CHUNK)
-                plane_cols = slice(side * V + c * CHUNK, side * V + (c + 1) * CHUNK)
+                codes = x_codes[z, side][:, c * CHUNK : (c + 1) * CHUNK]
+                plane = x_planes[PACK * z :, side * V + c * CHUNK : side * V + (c + 1) * CHUNK]
                 for t in range(PACK):
-                    nc.tensor.matmul_mx(
-                        hidden[c][:, t, :],
-                        lhsT=w_codes[:, t * P : (t + 1) * P].bitcast(FP8X4),
-                        lhsT_scale=w_plane[:, t * P : (t + 1) * P],
-                        rhs=x_codes[z, side][:, cols].bitcast(FP8X4),
-                        rhs_scale=x_planes[PACK * z :, plane_cols],
-                        start=(g == 0 and t == 0),
-                        stop=False,
-                    )
+                    multiply(hidden[c][:, t, :], w_mx, tile_cols[t], codes, plane, g == 0 and t == 0, False)
 
-        w3_codes = [codes_tile(P, "w3t%d" % t) for t in range(PACK)]
-        w3_planes = [plane_tile(P, "w3t%d" % t) for t in range(PACK)]
-        e_bf = {}
+        e_bf = [sb.tile([P, PACK * CHUNK], BF16, name="e_bf%d" % c, align_bytes=64) for c in range(N_CHUNKS)]
+        e_mx = [mx_tiles(CHUNK, "e%d" % c) for c in range(N_CHUNKS)]
+        w3_mx = [mx_tiles(P, "w3t%d" % t) for t in range(PACK)]
+        w3_bf = round_dealt(w3_raw, W3_VECTOR_SHARE, "w3_bf")
 
-        def round_edges(c):
-            copy = nc.scalar.copy if c in SCALAR_EDGE_CHUNKS else nc.vector.tensor_copy
-            e_bf[c] = round_plain(e_raw[c], CHUNK, "e%d" % c, copy)
+        def quantize_w3(t):
+            quantize(w3_bf[:, PACK * P * t : PACK * P * (t + 1)], w3_mx[t], whole)
 
-        e_mx = {}
-
-        def quantize_edges(c):
-            e_mx[c] = codes_tile(CHUNK, "e%d" % c), plane_tile(CHUNK, "e%d" % c)
-            quantize(e_bf[c][:], e_mx[c][0][:], e_mx[c][1][:])
-
-        grouped = round_dealt(w3_raw, W3_VECTOR_SHARE, "w3_bf")
-        round_edges(0)
-        for t in range(PACK):
-            quantize(grouped[:, t, :], w3_codes[t][:], w3_planes[t][:])
-        quantize_edges(0)
-
-        for c in range(N_CHUNKS):
-            if c + 1 < N_CHUNKS:
-                round_edges(c + 1)
-            if c > 0:
-                quantize_edges(c)
-            e_codes, e_plane = e_mx[c]
+        def edge_pass(c):
             for t in range(PACK):
-                nc.tensor.matmul_mx(
-                    hidden[c][:, t, :],
-                    lhsT=w3_codes[t][:].bitcast(FP8X4),
-                    lhsT_scale=w3_planes[t][:],
-                    rhs=e_codes[:].bitcast(FP8X4),
-                    rhs_scale=e_plane[:],
-                    start=False,
-                    stop=(t == PACK - 1),
-                )
+                multiply(hidden[c][:, t, :], w3_mx[t], whole, e_mx[c][0][:], e_mx[c][1][:], False, t == PACK - 1)
 
-        grouped = round_plain(w4_raw[:], N, "w4", nc.vector.tensor_copy)
-        w4_codes, w4_plane = codes_tile(N, "w4"), plane_tile(N, "w4")
-        quantize(grouped[:], w4_codes[:], w4_plane[:])
-        for c in range(N_CHUNKS):
-            h_bf = sb.tile([P, CHUNK * PACK], BF16, name="h_bf%d" % c, align_bytes=64)
+        quantize_w3(0)
+        quantize_w3(1)
+        round_plain(e_raw[0], e_bf[0], slice(0, FIRST_CHUNK_VECTOR), nc.vector.tensor_copy)
+        round_plain(e_raw[0], e_bf[0], slice(FIRST_CHUNK_VECTOR, CHUNK), nc.scalar.copy)
+        quantize_w3(2)
+        quantize(e_bf[0], e_mx[0], whole)
+        quantize_w3(3)
+        edge_pass(0)
+        round_plain(e_raw[1], e_bf[1], whole, nc.scalar.copy)
+        round_plain(e_raw[2], e_bf[2], low, nc.vector.tensor_copy)
+        round_plain(e_raw[2], e_bf[2], high, nc.scalar.copy)
+        for c in (1, 2):
+            quantize(e_bf[c], e_mx[c], whole)
+            edge_pass(c)
+        for half in (low, high):
+            round_plain(e_raw[LAST], e_bf[LAST], half, nc.vector.tensor_copy)
+        for half in (low, high):
+            quantize(e_bf[LAST], e_mx[LAST], half)
+        edge_pass(LAST)
+
+        w4_bf = sb.tile([P, PACK * N], BF16, name="w4_bf", align_bytes=64)
+        round_plain(w4_raw, w4_bf, slice(0, N), nc.vector.tensor_copy)
+        w4_mx = mx_tiles(N, "w4")
+        quantize(w4_bf, w4_mx, slice(0, N))
+
+        def second_layer(c, cols, result):
+            name = "h%d_%d" % (c, cols.start)
+            width = cols.stop - cols.start
+            if (c, cols) == (LAST, high):
+                h_bf = shared.tile([P, width * PACK], BF16, name=name + "_bf", align_bytes=64, offset=T)
+            elif (c, cols) == (LAST, low):
+                h_bf = shared.tile([P, width * PACK], BF16, name=name + "_bf", align_bytes=64, offset=T + 1024)
+            else:
+                h_bf = sb.tile([P, width * PACK], BF16, name=name + "_bf", align_bytes=64)
             nc.scalar.activation(
                 h_bf[:].rearrange("p (v t) -> p v t", t=PACK),
-                hidden[c][:].rearrange("p t v -> p v t"),
+                hidden[c][:, :, cols].rearrange("p t v -> p v t"),
                 GELU,
                 bias=gelu_bias[:],
             )
-            h_codes, h_plane = codes_tile(CHUNK, "h%d" % c), plane_tile(CHUNK, "h%d" % c)
-            quantize(h_bf[:], h_codes[:], h_plane[:])
-            result = ps.tile([N, CHUNK], F32, name="result%d" % c)
-            nc.tensor.matmul_mx(
-                result[:],
-                lhsT=w4_codes[:].bitcast(FP8X4),
-                lhsT_scale=w4_plane[:],
-                rhs=h_codes[:].bitcast(FP8X4),
-                rhs_scale=h_plane[:],
-                start=True,
-                stop=True,
-            )
-            staged = sb.tile([N, CHUNK], F32, name="staged%d" % c)
-            copy = nc.scalar.copy if c in SCALAR_RESULT_CHUNKS else nc.vector.tensor_copy
-            copy(staged[:], result[:])
-            nc.sync.dma_start(out[:, c * CHUNK : (c + 1) * CHUNK], staged[:])
+            h_mx = mx_tiles(width, name)
+            quantize(h_bf, h_mx, slice(0, width))
+            multiply(result, w4_mx, slice(0, N), h_mx[0][:], h_mx[1][:], True, True)
+
+        early = ps.tile([N, 2 * CHUNK], F32, name="early")
+        for c in range(2):
+            second_layer(c, whole, early[:, c * CHUNK : (c + 1) * CHUNK])
+        third = ps.tile([N, CHUNK], F32, name="third")
+        second_layer(2, whole, third[:])
+        late = [ps.tile([N, HALF], F32, name="late%d" % i) for i in range(2)]
+        second_layer(LAST, low, late[0][:])
+        second_layer(LAST, high, late[1][:])
+
+        staged = shared.tile([N, 2 * CHUNK], F32, name="staged01", align_bytes=64, offset=T + 1024)
+        nc.scalar.copy(staged[:], early[:])
+        nc.sync.dma_start(out[:, : 2 * CHUNK], staged[:])
+        staged = shared.tile([N, CHUNK], F32, name="staged2", align_bytes=64, offset=T)
+        nc.vector.tensor_copy(staged[:], third[:])
+        nc.sync.dma_start(out[:, 2 * CHUNK : 3 * CHUNK], staged[:])
+        staged = sb.tile([N, CHUNK], F32, name="staged3")
+        for i, half in enumerate((low, high)):
+            nc.vector.tensor_copy(staged[:, half], late[i][:])
+        nc.sync.dma_start(out[:, LAST * CHUNK :], staged[:])

@@ -28,6 +28,7 @@ SIDE_COLS = V // 16
 VECTOR_SHARE = (0, 32, 64, 80)
 W3_VECTOR_SHARE = 84
 FIRST_CHUNK_VECTOR = 96
+TABLE_AT = 8192
 EDGE_LOADS = ((0, 2), (2, 1), (3, 1))
 
 
@@ -40,8 +41,11 @@ def tile_picked_edgeup_gelu_p_kernel(tc, x_words, x_scales, eT, w1, w2, w3, w4, 
 
         offsets = sb.tile([P, 2 * SIDE_COLS], U16, name="offsets")
 
-        scale_table = shared.tile([P, T], U8, name="scale_table", align_bytes=64, offset=0)
+        scale_table = shared.tile([P, T], U8, name="scale_table", align_bytes=64, offset=TABLE_AT)
         nc.vector.memset(scale_table[:].bitcast(I32), 0)
+        x_planes = [sb.tile([P, 2 * V], U8, name="x_planes%d" % z, align_bytes=64) for z in range(2)]
+        for z in range(2):
+            nc.vector.memset(x_planes[z][:].bitcast(I32), 0)
         zero = sb.tile([P, 1], F32, name="zero")
         nc.vector.memset(zero[:], 0.0)
         gelu_bias = sb.tile([P, 1], F32, name="gelu_bias")
@@ -56,21 +60,27 @@ def tile_picked_edgeup_gelu_p_kernel(tc, x_words, x_scales, eT, w1, w2, w3, w4, 
             nc.sync.dma_start(table[:], x_words[z].rearrange("p n r -> p (n r)").bitcast(I32))
             return table
 
-        def load_scales(run):
-            for r in range(2 * run, 2 * run + 2):
-                for z in range(2):
-                    rows = x_scales[z, r::PACK, :]
-                    nc.sync.dma_start(scale_table[PACK * z + r :: QUADRANT, :].bitcast(I32), rows.bitcast(I32))
-
         word_tables = [load_words(0)]
         nc.sync.dma_start(offsets[:], offs)
-        load_scales(0)
+        scale_rows = x_scales.rearrange("z q n -> (z q) n").bitcast(I32)
+        nc.sync.dma_start(scale_table[::PACK, :].bitcast(I32), scale_rows)
         nc.scalar.activation(gelu_bias[:], zero[:], GELU)
         w_raw = [load_rows(w1[0:K_PASS, :], "w_raw0")]
-        load_scales(1)
         word_tables.append(load_words(1))
         w_raw.append(load_rows(w2[0:K_PASS, :], "w_raw1"))
+        picked_scales = sb.tile([P, 2 * V], U8, name="picked_scales", align_bytes=64)
+        nc.vector.tensor_copy(picked_scales[:], scale_table[:].indirect(offsets[:]))
+
+        def place_scales(z, r):
+            rows = picked_scales[64 * z + PACK * r : 64 * (z + 1) : 16, :]
+            nc.sync.dma_start(x_planes[z][PACK * z + r :: QUADRANT, :].bitcast(I32), rows.bitcast(I32))
+
+        moves = [(z, r) for z in range(2) for r in range(PACK)]
+        for z, r in moves[:6]:
+            place_scales(z, r)
         w_raw.append(load_rows(w1[K_PASS:K, :], "w_raw2"))
+        for z, r in moves[6:]:
+            place_scales(z, r)
         w_raw.append(load_rows(w2[K_PASS:K, :], "w_raw3"))
         w3_raw = load_rows(w3, "w3_raw")
         e_raw = []
@@ -80,7 +90,11 @@ def tile_picked_edgeup_gelu_p_kernel(tc, x_words, x_scales, eT, w1, w2, w3, w4, 
         w4_raw = load_rows(w4, "w4_raw")
 
         def gather_words(z, side):
-            picked = sb.tile([P, V], U32, name="x_codes%d%d" % (z, side), align_bytes=64)
+            if z == 0:
+                at = TABLE_AT - 4 * V + 64 if side == 0 else TABLE_AT + T - 64
+                picked = shared.tile([P, V], U32, name="x_codes0%d" % side, align_bytes=64, offset=at)
+            else:
+                picked = sb.tile([P, V], U32, name="x_codes%d%d" % (z, side), align_bytes=64)
             entries = offsets[:, side * SIDE_COLS : (side + 1) * SIDE_COLS]
             nc.vector.tensor_copy(picked[:], word_tables[z][:].bitcast(U32).indirect(entries))
             return picked
@@ -88,8 +102,6 @@ def tile_picked_edgeup_gelu_p_kernel(tc, x_words, x_scales, eT, w1, w2, w3, w4, 
         x_codes = {}
         x_codes[0, 0] = gather_words(0, 0)
         x_codes[0, 1] = gather_words(0, 1)
-        x_planes = sb.tile([P, 2 * V], U8, name="x_planes", align_bytes=64)
-        nc.vector.tensor_copy(x_planes[:], scale_table[:].indirect(offsets[:]))
         x_codes[1, 0] = gather_words(1, 0)
         x_codes[1, 1] = gather_words(1, 1)
 
@@ -133,15 +145,11 @@ def tile_picked_edgeup_gelu_p_kernel(tc, x_words, x_scales, eT, w1, w2, w3, w4, 
         for g in range(4):
             z, side = divmod(g, 2)
             grouped = round_dealt(w_raw[g], VECTOR_SHARE[g], "w_bf%d" % g)
-            if g == 0:
-                codes = sb.tile([P, H], U32, name="w0_codes", align_bytes=64)
-                w_mx = codes, shared.tile([P, H], U8, name="w0_plane", align_bytes=64, offset=0)
-            else:
-                w_mx = mx_tiles(H, "w%d" % g)
+            w_mx = mx_tiles(H, "w%d" % g)
             quantize(grouped, w_mx, slice(0, H))
             for c in range(N_CHUNKS):
                 codes = x_codes[z, side][:, c * CHUNK : (c + 1) * CHUNK]
-                plane = x_planes[PACK * z :, side * V + c * CHUNK : side * V + (c + 1) * CHUNK]
+                plane = x_planes[z][PACK * z :, side * V + c * CHUNK : side * V + (c + 1) * CHUNK]
                 for t in range(PACK):
                     multiply(hidden[c][:, t, :], w_mx, tile_cols[t], codes, plane, g == 0 and t == 0, False)
 

@@ -27,9 +27,10 @@ SIDE_COLS = V // 16
 
 VECTOR_SHARE = (0, 32, 64, 80)
 W3_VECTOR_SHARE = 84
-FIRST_CHUNK_VECTOR = 96
+FIRST_CHUNK_VECTOR = 80
 TABLE_AT = 8192
-EDGE_LOADS = ((0, 2), (2, 1), (3, 1))
+EDGE_LOADS = ((0, 2), (2, 1))
+LAST_AT = 12288
 
 
 def tile_picked_edgeup_gelu_p_kernel(tc, x_words, x_scales, eT, w1, w2, w3, w4, offs, out):
@@ -71,22 +72,28 @@ def tile_picked_edgeup_gelu_p_kernel(tc, x_words, x_scales, eT, w1, w2, w3, w4, 
         picked_scales = sb.tile([P, 2 * V], U8, name="picked_scales", align_bytes=64)
         nc.vector.tensor_copy(picked_scales[:], scale_table[:].indirect(offsets[:]))
 
-        def place_scales(z, r):
+        def place_scales(z, r, queue):
             rows = picked_scales[64 * z + PACK * r : 64 * (z + 1) : 16, :]
-            nc.sync.dma_start(x_planes[z][PACK * z + r :: QUADRANT, :].bitcast(I32), rows.bitcast(I32))
+            queue.dma_start(x_planes[z][PACK * z + r :: QUADRANT, :].bitcast(I32), rows.bitcast(I32))
 
         moves = [(z, r) for z in range(2) for r in range(PACK)]
         for z, r in moves[:6]:
-            place_scales(z, r)
+            place_scales(z, r, nc.sync)
         w_raw.append(load_rows(w1[K_PASS:K, :], "w_raw2"))
-        for z, r in moves[6:]:
-            place_scales(z, r)
+        place_scales(*moves[6], nc.sync)
+        place_scales(*moves[7], nc.gpsimd)
         w_raw.append(load_rows(w2[K_PASS:K, :], "w_raw3"))
         w3_raw = load_rows(w3, "w3_raw")
         e_raw = []
         for first, count in EDGE_LOADS:
             raw = load_rows(eT[:, first * CHUNK : (first + count) * CHUNK], "e_raw%d" % first)
             e_raw.extend(raw[:, :, i * CHUNK : (i + 1) * CHUNK] for i in range(count))
+        last_rows = eT[:, LAST * CHUNK :].rearrange("(p j) c -> p j c", j=PACK)
+        last_raw = []
+        for pair in range(2):
+            raw = shared.tile([P, 2, CHUNK], F32, name="e_last%d" % pair, align_bytes=64, offset=LAST_AT + 1024 * pair)
+            nc.sync.dma_start(raw[:], last_rows[:, 2 * pair : 2 * pair + 2, :])
+            last_raw.append(raw)
         w4_raw = load_rows(w4, "w4_raw")
 
         def gather_words(z, side):
@@ -176,13 +183,19 @@ def tile_picked_edgeup_gelu_p_kernel(tc, x_words, x_scales, eT, w1, w2, w3, w4, 
         round_plain(e_raw[1], e_bf[1], whole, nc.scalar.copy)
         round_plain(e_raw[2], e_bf[2], low, nc.vector.tensor_copy)
         round_plain(e_raw[2], e_bf[2], high, nc.scalar.copy)
-        for c in (1, 2):
-            quantize(e_bf[c], e_mx[c], whole)
-            edge_pass(c)
-        for half in (low, high):
-            round_plain(e_raw[LAST], e_bf[LAST], half, nc.vector.tensor_copy)
-        for half in (low, high):
-            quantize(e_bf[LAST], e_mx[LAST], half)
+        last_dst = e_bf[LAST][:].rearrange("p (c e j) -> p c j e", e=RUN, j=PACK)
+
+        def round_last(pair):
+            src = last_raw[pair][:].rearrange("p j (c e) -> p c j e", e=RUN)
+            nc.vector.tensor_copy(last_dst[:, :, 2 * pair : 2 * pair + 2, :], src)
+
+        quantize(e_bf[1], e_mx[1], whole)
+        edge_pass(1)
+        round_last(0)
+        quantize(e_bf[2], e_mx[2], whole)
+        edge_pass(2)
+        round_last(1)
+        quantize(e_bf[LAST], e_mx[LAST], whole)
         edge_pass(LAST)
 
         w4_bf = sb.tile([P, PACK * N], BF16, name="w4_bf", align_bytes=64)
@@ -205,7 +218,10 @@ def tile_picked_edgeup_gelu_p_kernel(tc, x_words, x_scales, eT, w1, w2, w3, w4, 
                 GELU,
                 bias=gelu_bias[:],
             )
-            h_mx = mx_tiles(width, name)
+            if c > 0:
+                h_mx = mx_tiles(width, name)
+            else:
+                h_mx = (sb.tile([P, width], U32, name="h0_codes", align_bytes=64), shared.tile([P, width], U8, name="h0_plane", align_bytes=64, offset=LAST_AT + 1024))
             quantize(h_bf, h_mx, slice(0, width))
             multiply(result, w4_mx, slice(0, N), h_mx[0][:], h_mx[1][:], True, True)
 

@@ -43,12 +43,12 @@ def tile_picked_edgeup_gelu_p_kernel(tc, x_words, x_scales, eT, w1, w2, w3, w4, 
         offsets = sb.tile([P, 2 * SIDE_COLS], U16, name="offsets")
 
         scale_table = shared.tile([P, T], U8, name="scale_table", align_bytes=64, offset=TABLE_AT)
-        nc.vector.memset(scale_table[:].bitcast(I32), 0)
+        nc.gpsimd.memset(scale_table[:].bitcast(I32), 0)
         x_planes = [sb.tile([P, 2 * V], U8, name="x_planes%d" % z, align_bytes=64) for z in range(2)]
         for z in range(2):
-            nc.vector.memset(x_planes[z][:].bitcast(I32), 0)
+            nc.gpsimd.memset(x_planes[z][:].bitcast(I32), 0)
         zero = sb.tile([P, 1], F32, name="zero")
-        nc.vector.memset(zero[:], 0.0)
+        nc.gpsimd.memset(zero[:], 0.0)
         gelu_bias = sb.tile([P, 1], F32, name="gelu_bias")
 
         def load_rows(rows, name):
@@ -154,10 +154,10 @@ def tile_picked_edgeup_gelu_p_kernel(tc, x_words, x_scales, eT, w1, w2, w3, w4, 
             grouped = round_dealt(w_raw[g], VECTOR_SHARE[g], "w_bf%d" % g)
             w_mx = mx_tiles(H, "w%d" % g)
             quantize(grouped, w_mx, slice(0, H))
-            for c in range(N_CHUNKS):
-                codes = x_codes[z, side][:, c * CHUNK : (c + 1) * CHUNK]
-                plane = x_planes[z][PACK * z :, side * V + c * CHUNK : side * V + (c + 1) * CHUNK]
-                for t in range(PACK):
+            for t in range(PACK):
+                for c in range(N_CHUNKS):
+                    codes = x_codes[z, side][:, c * CHUNK : (c + 1) * CHUNK]
+                    plane = x_planes[z][PACK * z :, side * V + c * CHUNK : side * V + (c + 1) * CHUNK]
                     multiply(hidden[c][:, t, :], w_mx, tile_cols[t], codes, plane, g == 0 and t == 0, False)
 
         e_bf = [sb.tile([P, PACK * CHUNK], BF16, name="e_bf%d" % c, align_bytes=64) for c in range(N_CHUNKS)]
@@ -185,17 +185,20 @@ def tile_picked_edgeup_gelu_p_kernel(tc, x_words, x_scales, eT, w1, w2, w3, w4, 
         round_plain(e_raw[2], e_bf[2], high, nc.scalar.copy)
         last_dst = e_bf[LAST][:].rearrange("p (c e j) -> p c j e", e=RUN, j=PACK)
 
-        def round_last(pair):
+        def round_last(pair, cols):
+            runs = slice(cols.start // RUN, cols.stop // RUN)
             src = last_raw[pair][:].rearrange("p j (c e) -> p c j e", e=RUN)
-            nc.vector.tensor_copy(last_dst[:, :, 2 * pair : 2 * pair + 2, :], src)
+            nc.vector.tensor_copy(last_dst[:, runs, 2 * pair : 2 * pair + 2, :], src[:, runs])
 
         quantize(e_bf[1], e_mx[1], whole)
         edge_pass(1)
-        round_last(0)
+        round_last(0, whole)
         quantize(e_bf[2], e_mx[2], whole)
         edge_pass(2)
-        round_last(1)
-        quantize(e_bf[LAST], e_mx[LAST], whole)
+        for half in (low, high):
+            round_last(1, half)
+        for half in (low, high):
+            quantize(e_bf[LAST], e_mx[LAST], half)
         edge_pass(LAST)
 
         w4_bf = sb.tile([P, PACK * N], BF16, name="w4_bf", align_bytes=64)

@@ -29,8 +29,10 @@ VECTOR_SHARE = (0, 32, 64, 80)
 W3_VECTOR_SHARE = 84
 FIRST_CHUNK_VECTOR = 80
 TABLE_AT = 8192
-EDGE_LOADS = ((0, 2), (2, 1))
+EDGE_LOADS = ((0, 0, 2, 0, 256), (0, 2, 4, 0, 256), (1, 0, 4, 0, 160), (1, 0, 2, 160, 256), (1, 2, 4, 160, 256))
+AHEAD = 32
 LAST_AT = 12288
+W4_AT = 16384
 
 
 def tile_picked_edgeup_gelu_p_kernel(tc, x_words, x_scales, eT, w1, w2, w3, w4, offs, out):
@@ -80,21 +82,20 @@ def tile_picked_edgeup_gelu_p_kernel(tc, x_words, x_scales, eT, w1, w2, w3, w4, 
         for z, r in moves[:6]:
             place_scales(z, r, nc.sync)
         w_raw.append(load_rows(w1[K_PASS:K, :], "w_raw2"))
-        place_scales(*moves[6], nc.sync)
+        place_scales(*moves[6], nc.gpsimd)
         place_scales(*moves[7], nc.gpsimd)
         w_raw.append(load_rows(w2[K_PASS:K, :], "w_raw3"))
         w3_raw = load_rows(w3, "w3_raw")
-        e_raw = []
-        for first, count in EDGE_LOADS:
-            raw = load_rows(eT[:, first * CHUNK : (first + count) * CHUNK], "e_raw%d" % first)
-            e_raw.extend(raw[:, :, i * CHUNK : (i + 1) * CHUNK] for i in range(count))
-        last_rows = eT[:, LAST * CHUNK :].rearrange("(p j) c -> p j c", j=PACK)
-        last_raw = []
-        for pair in range(2):
-            raw = shared.tile([P, 2, CHUNK], F32, name="e_last%d" % pair, align_bytes=64, offset=LAST_AT + 1024 * pair)
-            nc.sync.dma_start(raw[:], last_rows[:, 2 * pair : 2 * pair + 2, :])
-            last_raw.append(raw)
-        w4_raw = load_rows(w4, "w4_raw")
+        e_pairs = [
+            sb.tile([P, PACK, 2 * CHUNK], F32, name="e_raw01"),
+            shared.tile([P, PACK, 2 * CHUNK], F32, name="e_raw23", align_bytes=64, offset=LAST_AT),
+        ]
+        e_rows = eT.rearrange("(p j) c -> p j c", j=PACK)
+        for u, j0, j1, c0, c1 in EDGE_LOADS:
+            nc.sync.dma_start(e_pairs[u][:, j0:j1, c0:c1], e_rows[:, j0:j1, 256 * u + c0 : 256 * u + c1])
+        e_raw = [e_pairs[c // 2][:, :, (c % 2) * CHUNK : (c % 2 + 1) * CHUNK] for c in range(N_CHUNKS)]
+        w4_raw = shared.tile([P, PACK, N], F32, name="w4_raw", align_bytes=64, offset=W4_AT)
+        nc.sync.dma_start(w4_raw[:], w4.rearrange("(p j) c -> p j c", j=PACK))
 
         def gather_words(z, side):
             if z == 0:
@@ -141,9 +142,9 @@ def tile_picked_edgeup_gelu_p_kernel(tc, x_words, x_scales, eT, w1, w2, w3, w4, 
             nc.scalar.copy(dst[:, share:], src[:, share:])
             return grouped
 
-        def round_plain(raw, grouped, cols, copy):
+        def round_plain(raw, grouped, cols, copy, rows=slice(0, PACK)):
             dst = grouped[:, PACK * cols.start : PACK * cols.stop].rearrange("p (c e j) -> p c j e", e=RUN, j=PACK)
-            copy(dst, raw[:, :, cols].rearrange("p j (c e) -> p c j e", e=RUN))
+            copy(dst[:, :, rows, :], raw[:, rows, cols].rearrange("p j (c e) -> p c j e", e=RUN))
 
         tile_cols = [slice(t * P, (t + 1) * P) for t in range(PACK)]
         whole, low, high = slice(0, CHUNK), slice(0, HALF), slice(HALF, CHUNK)
@@ -172,10 +173,14 @@ def tile_picked_edgeup_gelu_p_kernel(tc, x_words, x_scales, eT, w1, w2, w3, w4, 
             for t in range(PACK):
                 multiply(hidden[c][:, t, :], w3_mx[t], whole, e_mx[c][0][:], e_mx[c][1][:], False, t == PACK - 1)
 
+        early_rows, late_rows = slice(0, 2), slice(2, PACK)
+        first, rest = slice(0, FIRST_CHUNK_VECTOR), slice(FIRST_CHUNK_VECTOR, CHUNK)
+        round_plain(e_raw[0], e_bf[0], first, nc.vector.tensor_copy, early_rows)
+        round_plain(e_raw[0], e_bf[0], rest, nc.scalar.copy, early_rows)
         quantize_w3(0)
         quantize_w3(1)
-        round_plain(e_raw[0], e_bf[0], slice(0, FIRST_CHUNK_VECTOR), nc.vector.tensor_copy)
-        round_plain(e_raw[0], e_bf[0], slice(FIRST_CHUNK_VECTOR, CHUNK), nc.scalar.copy)
+        round_plain(e_raw[0], e_bf[0], first, nc.vector.tensor_copy, late_rows)
+        round_plain(e_raw[0], e_bf[0], rest, nc.scalar.copy, late_rows)
         quantize_w3(2)
         quantize(e_bf[0], e_mx[0], whole)
         quantize_w3(3)
@@ -183,20 +188,14 @@ def tile_picked_edgeup_gelu_p_kernel(tc, x_words, x_scales, eT, w1, w2, w3, w4, 
         round_plain(e_raw[1], e_bf[1], whole, nc.scalar.copy)
         round_plain(e_raw[2], e_bf[2], low, nc.vector.tensor_copy)
         round_plain(e_raw[2], e_bf[2], high, nc.scalar.copy)
-        last_dst = e_bf[LAST][:].rearrange("p (c e j) -> p c j e", e=RUN, j=PACK)
-
-        def round_last(pair, cols):
-            runs = slice(cols.start // RUN, cols.stop // RUN)
-            src = last_raw[pair][:].rearrange("p j (c e) -> p c j e", e=RUN)
-            nc.vector.tensor_copy(last_dst[:, runs, 2 * pair : 2 * pair + 2, :], src[:, runs])
-
         quantize(e_bf[1], e_mx[1], whole)
         edge_pass(1)
-        round_last(0, whole)
+        round_plain(e_raw[LAST], e_bf[LAST], slice(0, AHEAD), nc.vector.tensor_copy)
+        round_plain(e_raw[LAST], e_bf[LAST], slice(AHEAD, CHUNK), nc.vector.tensor_copy, early_rows)
         quantize(e_bf[2], e_mx[2], whole)
         edge_pass(2)
-        for half in (low, high):
-            round_last(1, half)
+        for part in (slice(AHEAD, HALF), high):
+            round_plain(e_raw[LAST], e_bf[LAST], part, nc.vector.tensor_copy, late_rows)
         for half in (low, high):
             quantize(e_bf[LAST], e_mx[LAST], half)
         edge_pass(LAST)
@@ -221,10 +220,12 @@ def tile_picked_edgeup_gelu_p_kernel(tc, x_words, x_scales, eT, w1, w2, w3, w4, 
                 GELU,
                 bias=gelu_bias[:],
             )
-            if c > 0:
+            if c == LAST:
                 h_mx = mx_tiles(width, name)
             else:
-                h_mx = (sb.tile([P, width], U32, name="h0_codes", align_bytes=64), shared.tile([P, width], U8, name="h0_plane", align_bytes=64, offset=LAST_AT + 1024))
+                at = LAST_AT if c == 0 else W4_AT + CHUNK * c
+                codes = sb.tile([P, width], U32, name=name + "_codes", align_bytes=64)
+                h_mx = (codes, shared.tile([P, width], U8, name=name + "_plane", align_bytes=64, offset=at))
             quantize(h_bf, h_mx, slice(0, width))
             multiply(result, w4_mx, slice(0, N), h_mx[0][:], h_mx[1][:], True, True)
 

@@ -42,11 +42,11 @@ def tile_picked_edgeup_gelu_p_kernel(tc, x_words, x_scales, eT, w1, w2, w3, w4, 
         shared = ctx.enter_context(tc.tile_pool(name="shared", bufs=1))
         ps = ctx.enter_context(tc.psum_pool(name="ps", bufs=1))
 
-        offsets = sb.tile([P, 2 * SIDE_COLS], U16, name="offsets")
+        offsets = sb.tile([P, 2 * SIDE_COLS], U16, name="offsets", align_bytes=256)
 
-        scale_table = shared.tile([P, T], U8, name="scale_table", align_bytes=64, offset=TABLE_AT)
+        scale_table = shared.tile([P, T], U8, name="scale_table", align_bytes=256, offset=TABLE_AT)
         nc.gpsimd.memset(scale_table[:].bitcast(I32), 0)
-        x_planes = [sb.tile([P, 2 * V], U8, name="x_planes%d" % z, align_bytes=64) for z in range(2)]
+        x_planes = [sb.tile([P, 2 * V], U8, name="x_planes%d" % z, align_bytes=256) for z in range(2)]
         for z in range(2):
             nc.gpsimd.memset(x_planes[z][:].bitcast(I32), 0)
         zero = sb.tile([P, 1], F32, name="zero")
@@ -54,12 +54,12 @@ def tile_picked_edgeup_gelu_p_kernel(tc, x_words, x_scales, eT, w1, w2, w3, w4, 
         gelu_bias = sb.tile([P, 1], F32, name="gelu_bias")
 
         def load_rows(rows, name):
-            raw = sb.tile([P, PACK, rows.shape[1]], F32, name=name)
+            raw = sb.tile([P, PACK, rows.shape[1]], F32, name=name, align_bytes=256)
             nc.sync.dma_start(raw[:], rows.rearrange("(p j) c -> p j c", j=PACK))
             return raw
 
         def load_words(z):
-            table = sb.tile([P, T], I32, name="word_table%d" % z, align_bytes=64)
+            table = sb.tile([P, T], I32, name="word_table%d" % z, align_bytes=256)
             nc.sync.dma_start(table[:], x_words[z].rearrange("p n r -> p (n r)").bitcast(I32))
             return table
 
@@ -71,7 +71,7 @@ def tile_picked_edgeup_gelu_p_kernel(tc, x_words, x_scales, eT, w1, w2, w3, w4, 
         w_raw = [load_rows(w1[0:K_PASS, :], "w_raw0")]
         word_tables.append(load_words(1))
         w_raw.append(load_rows(w2[0:K_PASS, :], "w_raw1"))
-        picked_scales = sb.tile([P, 2 * V], U8, name="picked_scales", align_bytes=64)
+        picked_scales = sb.tile([P, 2 * V], U8, name="picked_scales", align_bytes=256)
         nc.vector.tensor_copy(picked_scales[:], scale_table[:].indirect(offsets[:]))
 
         def place_scales(z, r, queue):
@@ -87,14 +87,14 @@ def tile_picked_edgeup_gelu_p_kernel(tc, x_words, x_scales, eT, w1, w2, w3, w4, 
         w_raw.append(load_rows(w2[K_PASS:K, :], "w_raw3"))
         w3_raw = load_rows(w3, "w3_raw")
         e_pairs = [
-            sb.tile([P, PACK, 2 * CHUNK], F32, name="e_raw01"),
-            shared.tile([P, PACK, 2 * CHUNK], F32, name="e_raw23", align_bytes=64, offset=LAST_AT),
+            sb.tile([P, PACK, 2 * CHUNK], F32, name="e_raw01", align_bytes=256),
+            shared.tile([P, PACK, 2 * CHUNK], F32, name="e_raw23", align_bytes=256, offset=LAST_AT),
         ]
         e_rows = eT.rearrange("(p j) c -> p j c", j=PACK)
         for u, j0, j1, c0, c1 in EDGE_LOADS:
             nc.sync.dma_start(e_pairs[u][:, j0:j1, c0:c1], e_rows[:, j0:j1, 256 * u + c0 : 256 * u + c1])
         e_raw = [e_pairs[c // 2][:, :, (c % 2) * CHUNK : (c % 2 + 1) * CHUNK] for c in range(N_CHUNKS)]
-        w4_raw = shared.tile([P, PACK, N], F32, name="w4_raw", align_bytes=64, offset=W4_AT)
+        w4_raw = shared.tile([P, PACK, N], F32, name="w4_raw", align_bytes=256, offset=W4_AT)
         nc.sync.dma_start(w4_raw[:], w4.rearrange("(p j) c -> p j c", j=PACK))
 
         def gather_words(z, side):
@@ -244,7 +244,7 @@ def tile_picked_edgeup_gelu_p_kernel(tc, x_words, x_scales, eT, w1, w2, w3, w4, 
         staged = shared.tile([N, CHUNK], F32, name="staged2", align_bytes=64, offset=T)
         nc.vector.tensor_copy(staged[:], third[:])
         nc.sync.dma_start(out[:, 2 * CHUNK : 3 * CHUNK], staged[:])
-        staged = sb.tile([N, CHUNK], F32, name="staged3")
+        staged = sb.tile([N, CHUNK], F32, name="staged3", align_bytes=256)
         for i, half in enumerate((low, high)):
             nc.vector.tensor_copy(staged[:, half], late[i][:])
         nc.sync.dma_start(out[:, LAST * CHUNK :], staged[:])

@@ -22,17 +22,18 @@ QUADRANT = 32
 CHUNK = 128
 HALF = CHUNK // 2
 N_CHUNKS = V // CHUNK
-LAST = N_CHUNKS - 1
-SIDE_COLS = V // 16
 
-VECTOR_SHARE = (0, 32, 64, 80)
+VECTOR_SHARE = (0, 0, 64, 80)
 W3_VECTOR_SHARE = 84
 FIRST_CHUNK_VECTOR = 80
-TABLE_AT = 8192
-EDGE_LOADS = ((0, 0, 2, 0, 256), (0, 2, 4, 0, 256), (1, 0, 4, 0, 160), (1, 0, 2, 160, 256), (1, 2, 4, 160, 256))
 AHEAD = 32
-LAST_AT = 12288
-W4_AT = 16384
+SYNC_MOVES = 6
+
+SCALE_TABLE_AT = 0
+FIRST_CODES_AT = T - 64
+FIRST_EDGES_AT = 8192
+W4_AT = 12288
+LAST_H_AT = 16384
 
 
 def tile_picked_edgeup_gelu_p_kernel(tc, x_words, x_scales, eT, w1, w2, w3, w4, offs, out):
@@ -42,9 +43,9 @@ def tile_picked_edgeup_gelu_p_kernel(tc, x_words, x_scales, eT, w1, w2, w3, w4, 
         shared = ctx.enter_context(tc.tile_pool(name="shared", bufs=1))
         ps = ctx.enter_context(tc.psum_pool(name="ps", bufs=1))
 
-        offsets = sb.tile([P, 2 * SIDE_COLS], U16, name="offsets", align_bytes=256)
+        offsets = sb.tile([P, 2 * V // 16], U16, name="offsets", align_bytes=256)
 
-        scale_table = shared.tile([P, T], U8, name="scale_table", align_bytes=256, offset=TABLE_AT)
+        scale_table = shared.tile([P, T], U8, name="scale_table", align_bytes=256, offset=SCALE_TABLE_AT)
         nc.gpsimd.memset(scale_table[:].bitcast(I32), 0)
         x_planes = [sb.tile([P, 2 * V], U8, name="x_planes%d" % z, align_bytes=256) for z in range(2)]
         for z in range(2):
@@ -53,8 +54,9 @@ def tile_picked_edgeup_gelu_p_kernel(tc, x_words, x_scales, eT, w1, w2, w3, w4, 
         nc.gpsimd.memset(zero[:], 0.0)
         gelu_bias = sb.tile([P, 1], F32, name="gelu_bias")
 
-        def load_rows(rows, name):
-            raw = sb.tile([P, PACK, rows.shape[1]], F32, name=name, align_bytes=256)
+        def load_rows(rows, name, at=None):
+            pool = sb if at is None else shared
+            raw = pool.tile([P, PACK, rows.shape[1]], F32, name=name, align_bytes=256, offset=at)
             nc.sync.dma_start(raw[:], rows.rearrange("(p j) c -> p j c", j=PACK))
             return raw
 
@@ -79,48 +81,47 @@ def tile_picked_edgeup_gelu_p_kernel(tc, x_words, x_scales, eT, w1, w2, w3, w4, 
             queue.dma_start(x_planes[z][PACK * z + r :: QUADRANT, :].bitcast(I32), rows.bitcast(I32))
 
         moves = [(z, r) for z in range(2) for r in range(PACK)]
-        for z, r in moves[:6]:
+        for z, r in moves[:SYNC_MOVES]:
             place_scales(z, r, nc.sync)
         w_raw.append(load_rows(w1[K_PASS:K, :], "w_raw2"))
-        place_scales(*moves[6], nc.gpsimd)
-        place_scales(*moves[7], nc.gpsimd)
+        for z, r in moves[SYNC_MOVES:]:
+            place_scales(z, r, nc.gpsimd)
         w_raw.append(load_rows(w2[K_PASS:K, :], "w_raw3"))
         w3_raw = load_rows(w3, "w3_raw")
-        e_pairs = [
-            sb.tile([P, PACK, 2 * CHUNK], F32, name="e_raw01", align_bytes=256),
-            shared.tile([P, PACK, 2 * CHUNK], F32, name="e_raw23", align_bytes=256, offset=LAST_AT),
+
+        early_rows, late_rows, all_rows = slice(0, 2), slice(2, PACK), slice(0, PACK)
+        e_raw = [
+            shared.tile([P, PACK, 2 * CHUNK], F32, name="e_raw0", align_bytes=256, offset=FIRST_EDGES_AT),
+            sb.tile([P, PACK, 2 * CHUNK], F32, name="e_raw1", align_bytes=256),
         ]
         e_rows = eT.rearrange("(p j) c -> p j c", j=PACK)
-        for u, j0, j1, c0, c1 in EDGE_LOADS:
-            nc.sync.dma_start(e_pairs[u][:, j0:j1, c0:c1], e_rows[:, j0:j1, 256 * u + c0 : 256 * u + c1])
-        e_raw = [e_pairs[c // 2][:, :, (c % 2) * CHUNK : (c % 2 + 1) * CHUNK] for c in range(N_CHUNKS)]
-        w4_raw = shared.tile([P, PACK, N], F32, name="w4_raw", align_bytes=256, offset=W4_AT)
-        nc.sync.dma_start(w4_raw[:], w4.rearrange("(p j) c -> p j c", j=PACK))
 
-        def gather_words(z, side):
-            if z == 0:
-                at = TABLE_AT - 4 * V + 64 if side == 0 else TABLE_AT + T - 64
-                picked = shared.tile([P, V], U32, name="x_codes0%d" % side, align_bytes=64, offset=at)
-            else:
-                picked = sb.tile([P, V], U32, name="x_codes%d%d" % (z, side), align_bytes=64)
-            entries = offsets[:, side * SIDE_COLS : (side + 1) * SIDE_COLS]
-            nc.vector.tensor_copy(picked[:], word_tables[z][:].bitcast(U32).indirect(entries))
-            return picked
+        def load_edges(u, rows, cols):
+            first = 2 * CHUNK * u
+            nc.sync.dma_start(e_raw[u][:, rows, cols], e_rows[:, rows, first + cols.start : first + cols.stop])
 
-        x_codes = {}
-        x_codes[0, 0] = gather_words(0, 0)
-        x_codes[0, 1] = gather_words(0, 1)
-        x_codes[1, 0] = gather_words(1, 0)
-        x_codes[1, 1] = gather_words(1, 1)
+        third, tail = slice(0, CHUNK + AHEAD), slice(CHUNK + AHEAD, 2 * CHUNK)
+        load_edges(0, early_rows, slice(0, 2 * CHUNK))
+        load_edges(0, late_rows, slice(0, 2 * CHUNK))
+        load_edges(1, all_rows, third)
+        load_edges(1, early_rows, tail)
+        load_edges(1, late_rows, tail)
+        w4_raw = load_rows(w4, "w4_raw", W4_AT)
 
-        def mx_tiles(width, name):
-            codes = sb.tile([P, width], U32, name=name + "_codes", align_bytes=64)
+        x_codes = [
+            shared.tile([P, 2 * V], U32, name="x_codes0", align_bytes=64, offset=FIRST_CODES_AT),
+            sb.tile([P, 2 * V], U32, name="x_codes1", align_bytes=64),
+        ]
+        for z in range(2):
+            nc.vector.tensor_copy(x_codes[z][:], word_tables[z][:].bitcast(U32).indirect(offsets[:]))
+
+        def quantize(values, name, at=None):
+            width = values.shape[1] // PACK
+            pool = sb if at is None else shared
+            codes = pool.tile([P, width], U32, name=name + "_codes", align_bytes=64, offset=at)
             plane = sb.tile([P, width], U8, name=name + "_plane", align_bytes=64)
+            nc.vector.quantize_mx(codes[:].bitcast(FP8X4), plane[:], values)
             return codes, plane
-
-        def quantize(grouped, mx, cols):
-            values = grouped[:, PACK * cols.start : PACK * cols.stop]
-            nc.vector.quantize_mx(mx[0][:, cols].bitcast(FP8X4), mx[1][:, cols], values)
 
         def multiply(result, weights, w_cols, codes, plane, start, stop):
             nc.tensor.matmul_mx(
@@ -142,7 +143,7 @@ def tile_picked_edgeup_gelu_p_kernel(tc, x_words, x_scales, eT, w1, w2, w3, w4, 
             nc.scalar.copy(dst[:, share:], src[:, share:])
             return grouped
 
-        def round_plain(raw, grouped, cols, copy, rows=slice(0, PACK)):
+        def round_plain(raw, grouped, cols, copy, rows):
             dst = grouped[:, PACK * cols.start : PACK * cols.stop].rearrange("p (c e j) -> p c j e", e=RUN, j=PACK)
             copy(dst[:, :, rows, :], raw[:, rows, cols].rearrange("p j (c e) -> p c j e", e=RUN))
 
@@ -152,99 +153,76 @@ def tile_picked_edgeup_gelu_p_kernel(tc, x_words, x_scales, eT, w1, w2, w3, w4, 
         hidden = [ps.tile([P, PACK, CHUNK], F32, name="hidden%d" % c) for c in range(N_CHUNKS)]
         for g in range(4):
             z, side = divmod(g, 2)
-            grouped = round_dealt(w_raw[g], VECTOR_SHARE[g], "w_bf%d" % g)
-            w_mx = mx_tiles(H, "w%d" % g)
-            quantize(grouped, w_mx, slice(0, H))
+            w_mx = quantize(round_dealt(w_raw[g], VECTOR_SHARE[g], "w_bf%d" % g)[:], "w%d" % g)
             for t in range(PACK):
                 for c in range(N_CHUNKS):
-                    codes = x_codes[z, side][:, c * CHUNK : (c + 1) * CHUNK]
-                    plane = x_planes[z][PACK * z :, side * V + c * CHUNK : side * V + (c + 1) * CHUNK]
-                    multiply(hidden[c][:, t, :], w_mx, tile_cols[t], codes, plane, g == 0 and t == 0, False)
+                    entries = slice(side * V + c * CHUNK, side * V + (c + 1) * CHUNK)
+                    plane = x_planes[z][PACK * z :, entries]
+                    multiply(hidden[c][:, t, :], w_mx, tile_cols[t], x_codes[z][:, entries], plane, g == 0 and t == 0, False)
 
-        e_bf = [sb.tile([P, PACK * CHUNK], BF16, name="e_bf%d" % c, align_bytes=64) for c in range(N_CHUNKS)]
-        e_mx = [mx_tiles(CHUNK, "e%d" % c) for c in range(N_CHUNKS)]
-        w3_mx = [mx_tiles(P, "w3t%d" % t) for t in range(PACK)]
+        e_bf = [sb.tile([P, K_PASS], BF16, name="e_bf%d" % c, align_bytes=64) for c in range(2)]
         w3_bf = round_dealt(w3_raw, W3_VECTOR_SHARE, "w3_bf")
+        round_plain(e_raw[0], e_bf[0], whole, nc.scalar.copy, early_rows)
+        w3_first = quantize(w3_bf[:, : 3 * K_PASS], "w3_first")
+        round_plain(e_raw[0], e_bf[0], slice(0, FIRST_CHUNK_VECTOR), nc.vector.tensor_copy, late_rows)
+        round_plain(e_raw[0], e_bf[0], slice(FIRST_CHUNK_VECTOR, CHUNK), nc.scalar.copy, late_rows)
+        w3_last = quantize(w3_bf[:, 3 * K_PASS :], "w3_last")
+        w3_tiles = [(w3_first, tile_cols[t]) for t in range(3)] + [(w3_last, whole)]
 
-        def quantize_w3(t):
-            quantize(w3_bf[:, PACK * P * t : PACK * P * (t + 1)], w3_mx[t], whole)
+        def edge_pass(c, values):
+            codes, plane = quantize(values, "e%d" % c)
+            for t, (weights, cols) in enumerate(w3_tiles):
+                multiply(hidden[c][:, t, :], weights, cols, codes[:], plane[:], False, t == PACK - 1)
 
-        def edge_pass(c):
-            for t in range(PACK):
-                multiply(hidden[c][:, t, :], w3_mx[t], whole, e_mx[c][0][:], e_mx[c][1][:], False, t == PACK - 1)
-
-        early_rows, late_rows = slice(0, 2), slice(2, PACK)
-        first, rest = slice(0, FIRST_CHUNK_VECTOR), slice(FIRST_CHUNK_VECTOR, CHUNK)
-        round_plain(e_raw[0], e_bf[0], first, nc.vector.tensor_copy, early_rows)
-        round_plain(e_raw[0], e_bf[0], rest, nc.scalar.copy, early_rows)
-        quantize_w3(0)
-        quantize_w3(1)
-        round_plain(e_raw[0], e_bf[0], first, nc.vector.tensor_copy, late_rows)
-        round_plain(e_raw[0], e_bf[0], rest, nc.scalar.copy, late_rows)
-        quantize_w3(2)
-        quantize(e_bf[0], e_mx[0], whole)
-        quantize_w3(3)
-        edge_pass(0)
-        round_plain(e_raw[1], e_bf[1], whole, nc.scalar.copy)
-        round_plain(e_raw[2], e_bf[2], low, nc.vector.tensor_copy)
-        round_plain(e_raw[2], e_bf[2], high, nc.scalar.copy)
-        quantize(e_bf[1], e_mx[1], whole)
-        edge_pass(1)
-        round_plain(e_raw[LAST], e_bf[LAST], slice(0, AHEAD), nc.vector.tensor_copy)
-        round_plain(e_raw[LAST], e_bf[LAST], slice(AHEAD, CHUNK), nc.vector.tensor_copy, early_rows)
-        quantize(e_bf[2], e_mx[2], whole)
-        edge_pass(2)
-        for part in (slice(AHEAD, HALF), high):
-            round_plain(e_raw[LAST], e_bf[LAST], part, nc.vector.tensor_copy, late_rows)
-        for half in (low, high):
-            quantize(e_bf[LAST], e_mx[LAST], half)
-        edge_pass(LAST)
+        edge_pass(0, e_bf[0][:])
+        round_plain(e_raw[0][:, :, CHUNK:], e_bf[1], whole, nc.scalar.copy, all_rows)
+        edge_pass(1, e_bf[1][:])
+        e_bf23 = shared.tile([P, 2 * PACK * CHUNK], BF16, name="e_bf23", align_bytes=64, offset=FIRST_EDGES_AT)
+        round_plain(e_raw[1], e_bf23, third, nc.vector.tensor_copy, all_rows)
+        round_plain(e_raw[1], e_bf23, tail, nc.vector.tensor_copy, early_rows)
+        edge_pass(2, e_bf23[:, :K_PASS])
+        round_plain(e_raw[1], e_bf23, tail, nc.vector.tensor_copy, late_rows)
+        edge_pass(3, e_bf23[:, K_PASS:])
 
         w4_bf = sb.tile([P, PACK * N], BF16, name="w4_bf", align_bytes=64)
-        round_plain(w4_raw, w4_bf, slice(0, N), nc.vector.tensor_copy)
-        w4_mx = mx_tiles(N, "w4")
-        quantize(w4_bf, w4_mx, slice(0, N))
+        round_plain(w4_raw, w4_bf, slice(0, N), nc.vector.tensor_copy, all_rows)
 
-        def second_layer(c, cols, result):
-            name = "h%d_%d" % (c, cols.start)
-            width = cols.stop - cols.start
-            if (c, cols) == (LAST, high):
-                h_bf = shared.tile([P, width * PACK], BF16, name=name + "_bf", align_bytes=64, offset=T)
-            elif (c, cols) == (LAST, low):
-                h_bf = shared.tile([P, width * PACK], BF16, name=name + "_bf", align_bytes=64, offset=T + 1024)
-            else:
-                h_bf = sb.tile([P, width * PACK], BF16, name=name + "_bf", align_bytes=64)
+        def gelu(h_bf, c, cols):
             nc.scalar.activation(
-                h_bf[:].rearrange("p (v t) -> p v t", t=PACK),
+                h_bf.rearrange("p (v t) -> p v t", t=PACK),
                 hidden[c][:, :, cols].rearrange("p t v -> p v t"),
                 GELU,
                 bias=gelu_bias[:],
             )
-            if c == LAST:
-                h_mx = mx_tiles(width, name)
-            else:
-                at = LAST_AT if c == 0 else W4_AT + CHUNK * c
-                codes = sb.tile([P, width], U32, name=name + "_codes", align_bytes=64)
-                h_mx = (codes, shared.tile([P, width], U8, name=name + "_plane", align_bytes=64, offset=at))
-            quantize(h_bf, h_mx, slice(0, width))
-            multiply(result, w4_mx, slice(0, N), h_mx[0][:], h_mx[1][:], True, True)
 
-        early = ps.tile([N, 2 * CHUNK], F32, name="early")
+        def second_layer(h_mx, name):
+            result = ps.tile([N, h_mx[0].shape[1]], F32, name=name + "_result")
+            multiply(result[:], w4_mx, slice(0, N), h_mx[0][:], h_mx[1][:], True, True)
+            return result
+
+        h01 = sb.tile([P, 2 * K_PASS], BF16, name="h01_bf", align_bytes=64)
         for c in range(2):
-            second_layer(c, whole, early[:, c * CHUNK : (c + 1) * CHUNK])
-        third = ps.tile([N, CHUNK], F32, name="third")
-        second_layer(2, whole, third[:])
-        late = [ps.tile([N, HALF], F32, name="late%d" % i) for i in range(2)]
-        second_layer(LAST, low, late[0][:])
-        second_layer(LAST, high, late[1][:])
+            gelu(h01[:, c * K_PASS : (c + 1) * K_PASS], c, whole)
+        h01_mx = quantize(h01[:], "h01", W4_AT)
+        w4_mx = quantize(w4_bf[:], "w4")
+        result01 = second_layer(h01_mx, "h01")
+        h2 = sb.tile([P, K_PASS], BF16, name="h2_bf", align_bytes=64)
+        gelu(h2[:], 2, whole)
+        result2 = second_layer(quantize(h2[:], "h2"), "h2")
+        h3_low = shared.tile([P, PACK * HALF], BF16, name="h3_low_bf", align_bytes=64, offset=LAST_H_AT)
+        gelu(h3_low[:], 3, low)
+        result3_low = second_layer(quantize(h3_low[:], "h3_low"), "h3_low")
+        h3_high = shared.tile([P, PACK * HALF], BF16, name="h3_high_bf", align_bytes=64, offset=LAST_H_AT + 1024)
+        gelu(h3_high[:], 3, high)
+        result3_high = second_layer(quantize(h3_high[:], "h3_high"), "h3_high")
 
-        staged = shared.tile([N, 2 * CHUNK], F32, name="staged01", align_bytes=64, offset=T + 1024)
-        nc.scalar.copy(staged[:], early[:])
-        nc.sync.dma_start(out[:, : 2 * CHUNK], staged[:])
-        staged = shared.tile([N, CHUNK], F32, name="staged2", align_bytes=64, offset=T)
-        nc.vector.tensor_copy(staged[:], third[:])
-        nc.sync.dma_start(out[:, 2 * CHUNK : 3 * CHUNK], staged[:])
-        staged = sb.tile([N, CHUNK], F32, name="staged3", align_bytes=256)
-        for i, half in enumerate((low, high)):
-            nc.vector.tensor_copy(staged[:, half], late[i][:])
-        nc.sync.dma_start(out[:, LAST * CHUNK :], staged[:])
+        staged01 = shared.tile([N, 2 * CHUNK], F32, name="staged01", align_bytes=256, offset=LAST_H_AT - 768)
+        nc.scalar.copy(staged01[:], result01[:])
+        nc.sync.dma_start(out[:, : 2 * CHUNK], staged01[:])
+        staged2 = shared.tile([N, CHUNK], F32, name="staged2", align_bytes=256, offset=LAST_H_AT + 1024)
+        nc.vector.tensor_copy(staged2[:], result2[:])
+        nc.sync.dma_start(out[:, 2 * CHUNK : 3 * CHUNK], staged2[:])
+        staged3 = sb.tile([N, CHUNK], F32, name="staged3", align_bytes=256)
+        nc.scalar.copy(staged3[:, low], result3_low[:])
+        nc.vector.tensor_copy(staged3[:, high], result3_high[:])
+        nc.sync.dma_start(out[:, 3 * CHUNK :], staged3[:])

@@ -24,14 +24,10 @@ HALF = CHUNK // 2
 N_CHUNKS = V // CHUNK
 
 VECTOR_SHARE = (0, 0, 64, 80)
-W3_VECTOR_SHARE = 84
-FIRST_CHUNK_VECTOR = 80
-AHEAD = 32
 SYNC_MOVES = 6
 
 SCALE_TABLE_AT = 0
 FIRST_CODES_AT = T - 64
-FIRST_EDGES_AT = 8192
 W4_AT = 12288
 LAST_H_AT = 16384
 
@@ -89,23 +85,7 @@ def tile_picked_edgeup_gelu_p_kernel(tc, x_words, x_scales, eT, w1, w2, w3, w4, 
         w_raw.append(load_rows(w2[K_PASS:K, :], "w_raw3"))
         w3_raw = load_rows(w3, "w3_raw")
 
-        early_rows, late_rows, all_rows = slice(0, 2), slice(2, PACK), slice(0, PACK)
-        e_raw = [
-            shared.tile([P, PACK, 2 * CHUNK], F32, name="e_raw0", align_bytes=256, offset=FIRST_EDGES_AT),
-            sb.tile([P, PACK, 2 * CHUNK], F32, name="e_raw1", align_bytes=256),
-        ]
-        e_rows = eT.rearrange("(p j) c -> p j c", j=PACK)
-
-        def load_edges(u, rows, cols):
-            first = 2 * CHUNK * u
-            nc.sync.dma_start(e_raw[u][:, rows, cols], e_rows[:, rows, first + cols.start : first + cols.stop])
-
-        third, tail = slice(0, CHUNK + AHEAD), slice(CHUNK + AHEAD, 2 * CHUNK)
-        load_edges(0, early_rows, slice(0, 2 * CHUNK))
-        load_edges(0, late_rows, slice(0, 2 * CHUNK))
-        load_edges(1, all_rows, third)
-        load_edges(1, early_rows, tail)
-        load_edges(1, late_rows, tail)
+        e_raw = [load_rows(eT[:, c * CHUNK : (c + 1) * CHUNK], "e_raw%d" % c) for c in range(N_CHUNKS)]
         w4_raw = load_rows(w4, "w4_raw", W4_AT)
 
         x_codes = [
@@ -143,9 +123,9 @@ def tile_picked_edgeup_gelu_p_kernel(tc, x_words, x_scales, eT, w1, w2, w3, w4, 
             nc.scalar.copy(dst[:, share:], src[:, share:])
             return grouped
 
-        def round_plain(raw, grouped, cols, copy, rows):
-            dst = grouped[:, PACK * cols.start : PACK * cols.stop].rearrange("p (c e j) -> p c j e", e=RUN, j=PACK)
-            copy(dst[:, :, rows, :], raw[:, rows, cols].rearrange("p j (c e) -> p c j e", e=RUN))
+        def round_plain(raw, grouped, copy):
+            dst = grouped[:].rearrange("p (c e j) -> p c j e", e=RUN, j=PACK)
+            copy(dst, raw[:].rearrange("p j (c e) -> p c j e", e=RUN))
 
         tile_cols = [slice(t * P, (t + 1) * P) for t in range(PACK)]
         whole, low, high = slice(0, CHUNK), slice(0, HALF), slice(HALF, CHUNK)
@@ -160,32 +140,34 @@ def tile_picked_edgeup_gelu_p_kernel(tc, x_words, x_scales, eT, w1, w2, w3, w4, 
                     plane = x_planes[z][PACK * z :, entries]
                     multiply(hidden[c][:, t, :], w_mx, tile_cols[t], x_codes[z][:, entries], plane, g == 0 and t == 0, False)
 
-        e_bf = [sb.tile([P, K_PASS], BF16, name="e_bf%d" % c, align_bytes=64) for c in range(2)]
-        w3_bf = round_dealt(w3_raw, W3_VECTOR_SHARE, "w3_bf")
-        round_plain(e_raw[0], e_bf[0], whole, nc.scalar.copy, early_rows)
-        w3_first = quantize(w3_bf[:, : 3 * K_PASS], "w3_first")
-        round_plain(e_raw[0], e_bf[0], slice(0, FIRST_CHUNK_VECTOR), nc.vector.tensor_copy, late_rows)
-        round_plain(e_raw[0], e_bf[0], slice(FIRST_CHUNK_VECTOR, CHUNK), nc.scalar.copy, late_rows)
-        w3_last = quantize(w3_bf[:, 3 * K_PASS :], "w3_last")
-        w3_tiles = [(w3_first, tile_cols[t]) for t in range(3)] + [(w3_last, whole)]
+        def round_pair(pair, copy):
+            grouped = sb.tile([P, 2 * K_PASS], BF16, name="w3_bf%d" % pair, align_bytes=64)
+            src = w3_raw[:].rearrange("p j (m t) -> p m j t", t=PACK)[:, :, :, 2 * pair : 2 * pair + 2]
+            copy(grouped[:].rearrange("p (t m j) -> p m j t", t=2, j=PACK), src)
+            return grouped
 
-        def edge_pass(c, values):
-            codes, plane = quantize(values, "e%d" % c)
-            for t, (weights, cols) in enumerate(w3_tiles):
-                multiply(hidden[c][:, t, :], weights, cols, codes[:], plane[:], False, t == PACK - 1)
+        def round_edges(c, copy):
+            grouped = sb.tile([P, K_PASS], BF16, name="e_bf%d" % c, align_bytes=64)
+            round_plain(e_raw[c], grouped, copy)
+            return grouped
 
-        edge_pass(0, e_bf[0][:])
-        round_plain(e_raw[0][:, :, CHUNK:], e_bf[1], whole, nc.scalar.copy, all_rows)
-        edge_pass(1, e_bf[1][:])
-        e_bf23 = shared.tile([P, 2 * PACK * CHUNK], BF16, name="e_bf23", align_bytes=64, offset=FIRST_EDGES_AT)
-        round_plain(e_raw[1], e_bf23, third, nc.vector.tensor_copy, all_rows)
-        round_plain(e_raw[1], e_bf23, tail, nc.vector.tensor_copy, early_rows)
-        edge_pass(2, e_bf23[:, :K_PASS])
-        round_plain(e_raw[1], e_bf23, tail, nc.vector.tensor_copy, late_rows)
-        edge_pass(3, e_bf23[:, K_PASS:])
+        def edge_pass(c, e_mx):
+            for t in range(PACK):
+                multiply(hidden[c][:, t, :], w3_mx[t // 2], tile_cols[t % 2], e_mx[0][:], e_mx[1][:], False, t == PACK - 1)
+
+        w3_bf = [round_pair(0, nc.vector.tensor_copy), round_pair(1, nc.scalar.copy)]
+        e_bf = round_edges(0, nc.vector.tensor_copy)
+        w3_mx = [quantize(w3_bf[0][:], "w3_0")]
+        e_mx = quantize(e_bf[:], "e0")
+        w3_mx.append(quantize(w3_bf[1][:], "w3_1"))
+        edge_pass(0, e_mx)
+        edge_pass(1, quantize(round_edges(1, nc.scalar.copy)[:], "e1"))
+        for c in (2, 3):
+            edge_pass(c, quantize(round_edges(c, nc.vector.tensor_copy)[:], "e%d" % c))
 
         w4_bf = sb.tile([P, PACK * N], BF16, name="w4_bf", align_bytes=64)
-        round_plain(w4_raw, w4_bf, slice(0, N), nc.vector.tensor_copy, all_rows)
+        round_plain(w4_raw, w4_bf, nc.vector.tensor_copy)
+        w4_mx = quantize(w4_bf[:], "w4")
 
         def gelu(h_bf, c, cols):
             nc.scalar.activation(
@@ -204,7 +186,6 @@ def tile_picked_edgeup_gelu_p_kernel(tc, x_words, x_scales, eT, w1, w2, w3, w4, 
         for c in range(2):
             gelu(h01[:, c * K_PASS : (c + 1) * K_PASS], c, whole)
         h01_mx = quantize(h01[:], "h01", W4_AT)
-        w4_mx = quantize(w4_bf[:], "w4")
         result01 = second_layer(h01_mx, "h01")
         h2 = sb.tile([P, K_PASS], BF16, name="h2_bf", align_bytes=64)
         gelu(h2[:], 2, whole)

@@ -24,7 +24,8 @@ HALF = CHUNK // 2
 N_CHUNKS = V // CHUNK
 
 VECTOR_SHARE = (0, 0, 64, 80)
-SYNC_MOVES = 6
+SECOND_VECTOR = 32
+THIRD_VECTOR = 80
 
 SCALE_TABLE_AT = 0
 FIRST_CODES_AT = T - 64
@@ -43,9 +44,7 @@ def tile_picked_edgeup_gelu_p_kernel(tc, x_words, x_scales, eT, w1, w2, w3, w4, 
 
         scale_table = shared.tile([P, T], U8, name="scale_table", align_bytes=256, offset=SCALE_TABLE_AT)
         nc.gpsimd.memset(scale_table[:].bitcast(I32), 0)
-        x_planes = [sb.tile([P, 2 * V], U8, name="x_planes%d" % z, align_bytes=256) for z in range(2)]
-        for z in range(2):
-            nc.gpsimd.memset(x_planes[z][:].bitcast(I32), 0)
+        x_planes = sb.tile([P, 2 * V], U8, name="x_planes", align_bytes=256)
         zero = sb.tile([P, 1], F32, name="zero")
         nc.gpsimd.memset(zero[:], 0.0)
         gelu_bias = sb.tile([P, 1], F32, name="gelu_bias")
@@ -63,29 +62,29 @@ def tile_picked_edgeup_gelu_p_kernel(tc, x_words, x_scales, eT, w1, w2, w3, w4, 
 
         word_tables = [load_words(0)]
         nc.sync.dma_start(offsets[:], offs)
-        scale_rows = x_scales.rearrange("z q n -> (z q) n").bitcast(I32)
-        nc.sync.dma_start(scale_table[::PACK, :].bitcast(I32), scale_rows)
+        nc.sync.dma_start(scale_table[::PACK, :].bitcast(I32), x_scales.rearrange("z q n -> q z n").bitcast(I32))
         nc.scalar.activation(gelu_bias[:], zero[:], GELU)
         w_raw = [load_rows(w1[0:K_PASS, :], "w_raw0")]
         word_tables.append(load_words(1))
         w_raw.append(load_rows(w2[0:K_PASS, :], "w_raw1"))
         picked_scales = sb.tile([P, 2 * V], U8, name="picked_scales", align_bytes=256)
         nc.vector.tensor_copy(picked_scales[:], scale_table[:].indirect(offsets[:]))
+        nc.vector.tensor_copy(x_planes[:].bitcast(I32), picked_scales[:].bitcast(I32))
 
-        def place_scales(z, r, queue):
-            rows = picked_scales[64 * z + PACK * r : 64 * (z + 1) : 16, :]
-            queue.dma_start(x_planes[z][PACK * z + r :: QUADRANT, :].bitcast(I32), rows.bitcast(I32))
-
-        moves = [(z, r) for z in range(2) for r in range(PACK)]
-        for z, r in moves[:SYNC_MOVES]:
-            place_scales(z, r, nc.sync)
+        for z in range(2):
+            for r in range(1, PACK):
+                rows = picked_scales[PACK * z + 8 * r :: QUADRANT, :]
+                nc.sync.dma_start(x_planes[PACK * z + r :: QUADRANT, :].bitcast(I32), rows.bitcast(I32))
         w_raw.append(load_rows(w1[K_PASS:K, :], "w_raw2"))
-        for z, r in moves[SYNC_MOVES:]:
-            place_scales(z, r, nc.gpsimd)
         w_raw.append(load_rows(w2[K_PASS:K, :], "w_raw3"))
         w3_raw = load_rows(w3, "w3_raw")
 
-        e_raw = [load_rows(eT[:, c * CHUNK : (c + 1) * CHUNK], "e_raw%d" % c) for c in range(N_CHUNKS)]
+        e_raw = [load_rows(eT[:, c * CHUNK : (c + 1) * CHUNK], "e_raw%d" % c) for c in range(N_CHUNKS - 1)]
+        early_rows, late_rows = slice(0, 2), slice(2, PACK)
+        last_raw = sb.tile([P, PACK, CHUNK], F32, name="last_raw", align_bytes=256)
+        last_rows = eT[:, V - CHUNK :].rearrange("(p j) c -> p j c", j=PACK)
+        for rows in (early_rows, late_rows):
+            nc.sync.dma_start(last_raw[:, rows, :], last_rows[:, rows, :])
         w4_raw = load_rows(w4, "w4_raw", W4_AT)
 
         x_codes = [
@@ -123,9 +122,9 @@ def tile_picked_edgeup_gelu_p_kernel(tc, x_words, x_scales, eT, w1, w2, w3, w4, 
             nc.scalar.copy(dst[:, share:], src[:, share:])
             return grouped
 
-        def round_plain(raw, grouped, copy):
+        def round_plain(raw, grouped, copy, rows=slice(0, PACK)):
             dst = grouped[:].rearrange("p (c e j) -> p c j e", e=RUN, j=PACK)
-            copy(dst, raw[:].rearrange("p j (c e) -> p c j e", e=RUN))
+            copy(dst[:, :, rows, :], raw[:, rows, :].rearrange("p j (c e) -> p c j e", e=RUN))
 
         tile_cols = [slice(t * P, (t + 1) * P) for t in range(PACK)]
         whole, low, high = slice(0, CHUNK), slice(0, HALF), slice(HALF, CHUNK)
@@ -137,7 +136,7 @@ def tile_picked_edgeup_gelu_p_kernel(tc, x_words, x_scales, eT, w1, w2, w3, w4, 
             for t in range(PACK):
                 for c in range(N_CHUNKS):
                     entries = slice(side * V + c * CHUNK, side * V + (c + 1) * CHUNK)
-                    plane = x_planes[z][PACK * z :, entries]
+                    plane = x_planes[PACK * z :, entries]
                     multiply(hidden[c][:, t, :], w_mx, tile_cols[t], x_codes[z][:, entries], plane, g == 0 and t == 0, False)
 
         def round_pair(pair, copy):
@@ -146,24 +145,39 @@ def tile_picked_edgeup_gelu_p_kernel(tc, x_words, x_scales, eT, w1, w2, w3, w4, 
             copy(grouped[:].rearrange("p (t m j) -> p m j t", t=2, j=PACK), src)
             return grouped
 
-        def round_edges(c, copy):
-            grouped = sb.tile([P, K_PASS], BF16, name="e_bf%d" % c, align_bytes=64)
-            round_plain(e_raw[c], grouped, copy)
-            return grouped
+        e_bf = [sb.tile([P, K_PASS], BF16, name="e_bf%d" % c, align_bytes=64) for c in range(N_CHUNKS - 1)]
+
+        def round_edges(c, cols, copy):
+            round_plain(e_raw[c][:, :, cols], e_bf[c][:, PACK * cols.start : PACK * cols.stop], copy)
 
         def edge_pass(c, e_mx):
             for t in range(PACK):
                 multiply(hidden[c][:, t, :], w3_mx[t // 2], tile_cols[t % 2], e_mx[0][:], e_mx[1][:], False, t == PACK - 1)
 
         w3_bf = [round_pair(0, nc.vector.tensor_copy), round_pair(1, nc.scalar.copy)]
-        e_bf = round_edges(0, nc.vector.tensor_copy)
+        round_edges(0, whole, nc.vector.tensor_copy)
         w3_mx = [quantize(w3_bf[0][:], "w3_0")]
-        e_mx = quantize(e_bf[:], "e0")
+        e_mx = quantize(e_bf[0][:], "e0")
+        round_edges(1, slice(0, SECOND_VECTOR), nc.vector.tensor_copy)
+        round_edges(1, slice(SECOND_VECTOR, CHUNK), nc.scalar.copy)
         w3_mx.append(quantize(w3_bf[1][:], "w3_1"))
         edge_pass(0, e_mx)
-        edge_pass(1, quantize(round_edges(1, nc.scalar.copy)[:], "e1"))
-        for c in (2, 3):
-            edge_pass(c, quantize(round_edges(c, nc.vector.tensor_copy)[:], "e%d" % c))
+        edge_pass(1, quantize(e_bf[1][:], "e1"))
+        round_edges(2, slice(0, THIRD_VECTOR), nc.vector.tensor_copy)
+        round_edges(2, slice(THIRD_VECTOR, CHUNK), nc.scalar.copy)
+        last_bf = sb.tile([P, K_PASS], BF16, name="last_bf", align_bytes=64)
+        round_plain(last_raw, last_bf, nc.vector.tensor_copy, early_rows)
+        edge_pass(2, quantize(e_bf[2][:], "e2"))
+        last_values = [last_bf[:, PACK * half.start : PACK * half.stop] for half in (low, high)]
+        last_mx = (
+            sb.tile([P, CHUNK], U32, name="e3_codes", align_bytes=64),
+            sb.tile([P, CHUNK], U8, name="e3_plane", align_bytes=64),
+        )
+        for values, half in zip(last_values, (low, high)):
+            round_plain(last_raw[:, :, half], values, nc.vector.tensor_copy, late_rows)
+        for values, half in zip(last_values, (low, high)):
+            nc.vector.quantize_mx(last_mx[0][:, half].bitcast(FP8X4), last_mx[1][:, half], values[:])
+        edge_pass(3, last_mx)
 
         w4_bf = sb.tile([P, PACK * N], BF16, name="w4_bf", align_bytes=64)
         round_plain(w4_raw, w4_bf, nc.vector.tensor_copy)
@@ -189,7 +203,7 @@ def tile_picked_edgeup_gelu_p_kernel(tc, x_words, x_scales, eT, w1, w2, w3, w4, 
         result01 = second_layer(h01_mx, "h01")
         h2 = sb.tile([P, K_PASS], BF16, name="h2_bf", align_bytes=64)
         gelu(h2[:], 2, whole)
-        result2 = second_layer(quantize(h2[:], "h2"), "h2")
+        result2 = second_layer(quantize(h2[:], "h2", W4_AT + 1024), "h2")
         h3_low = shared.tile([P, PACK * HALF], BF16, name="h3_low_bf", align_bytes=64, offset=LAST_H_AT)
         gelu(h3_low[:], 3, low)
         result3_low = second_layer(quantize(h3_low[:], "h3_low"), "h3_low")

@@ -22,6 +22,7 @@ QUADRANT = 32
 CHUNK = 128
 HALF = CHUNK // 2
 N_CHUNKS = V // CHUNK
+LIST = 2 * V
 
 VECTOR_SHARE = (0, 0, 64, 80)
 SECOND_VECTOR = 32
@@ -44,7 +45,7 @@ def tile_picked_edgeup_gelu_p_kernel(tc, x_words, x_scales, eT, w1, w2, w3, w4, 
 
         scale_table = shared.tile([P, T], U8, name="scale_table", align_bytes=256, offset=SCALE_TABLE_AT)
         nc.gpsimd.memset(scale_table[:].bitcast(I32), 0)
-        x_planes = sb.tile([P, 2 * V], U8, name="x_planes", align_bytes=256)
+        x_planes = sb.tile([P, 2 * LIST], U8, name="x_planes", align_bytes=256)
         zero = sb.tile([P, 1], F32, name="zero")
         nc.gpsimd.memset(zero[:], 0.0)
         gelu_bias = sb.tile([P, 1], F32, name="gelu_bias")
@@ -69,12 +70,14 @@ def tile_picked_edgeup_gelu_p_kernel(tc, x_words, x_scales, eT, w1, w2, w3, w4, 
         w_raw.append(load_rows(w2[0:K_PASS, :], "w_raw1"))
         picked_scales = sb.tile([P, 2 * V], U8, name="picked_scales", align_bytes=256)
         nc.vector.tensor_copy(picked_scales[:], scale_table[:].indirect(offsets[:]))
-        nc.vector.tensor_copy(x_planes[:].bitcast(I32), picked_scales[:].bitcast(I32))
+        twice = picked_scales[:].bitcast(I32).unsqueeze(1).to_broadcast([P, 2, LIST // 4])
+        nc.vector.tensor_copy(x_planes[:].bitcast(I32).rearrange("p (z n) -> p z n", z=2), twice)
 
-        for z in range(2):
+        for z, queue in enumerate((nc.sync, nc.gpsimd)):
             for r in range(1, PACK):
                 rows = picked_scales[PACK * z + 8 * r :: QUADRANT, :]
-                nc.sync.dma_start(x_planes[PACK * z + r :: QUADRANT, :].bitcast(I32), rows.bitcast(I32))
+                place = x_planes[PACK * z + r :: QUADRANT, z * LIST : (z + 1) * LIST]
+                queue.dma_start(place.bitcast(I32), rows.bitcast(I32))
         w_raw.append(load_rows(w1[K_PASS:K, :], "w_raw2"))
         w_raw.append(load_rows(w2[K_PASS:K, :], "w_raw3"))
         w3_raw = load_rows(w3, "w3_raw")
@@ -136,7 +139,7 @@ def tile_picked_edgeup_gelu_p_kernel(tc, x_words, x_scales, eT, w1, w2, w3, w4, 
             for t in range(PACK):
                 for c in range(N_CHUNKS):
                     entries = slice(side * V + c * CHUNK, side * V + (c + 1) * CHUNK)
-                    plane = x_planes[PACK * z :, entries]
+                    plane = x_planes[PACK * z :, z * LIST + entries.start : z * LIST + entries.stop]
                     multiply(hidden[c][:, t, :], w_mx, tile_cols[t], x_codes[z][:, entries], plane, g == 0 and t == 0, False)
 
         def round_pair(pair, copy):

@@ -25,7 +25,7 @@ N_CHUNKS = V // CHUNK
 LIST = 2 * V
 
 VECTOR_SHARE = (0, 0, 64, 80)
-SECOND_VECTOR = 32
+SECOND_VECTOR = 16
 THIRD_VECTOR = 80
 
 SCALE_TABLE_AT = 0
@@ -73,10 +73,11 @@ def tile_picked_edgeup_gelu_p_kernel(tc, x_words, x_scales, eT, w1, w2, w3, w4, 
         twice = picked_scales[:].bitcast(I32).unsqueeze(1).to_broadcast([P, 2, LIST // 4])
         nc.vector.tensor_copy(x_planes[:].bitcast(I32).rearrange("p (z n) -> p z n", z=2), twice)
 
-        for z, queue in enumerate((nc.sync, nc.gpsimd)):
+        for z in range(2):
             for r in range(1, PACK):
                 rows = picked_scales[PACK * z + 8 * r :: QUADRANT, :]
                 place = x_planes[PACK * z + r :: QUADRANT, z * LIST : (z + 1) * LIST]
+                queue = nc.gpsimd if (z, r) == (1, PACK - 1) else nc.sync
                 queue.dma_start(place.bitcast(I32), rows.bitcast(I32))
         w_raw.append(load_rows(w1[K_PASS:K, :], "w_raw2"))
         w_raw.append(load_rows(w2[K_PASS:K, :], "w_raw3"))
@@ -210,15 +211,15 @@ def tile_picked_edgeup_gelu_p_kernel(tc, x_words, x_scales, eT, w1, w2, w3, w4, 
         h3_low = shared.tile([P, PACK * HALF], BF16, name="h3_low_bf", align_bytes=64, offset=LAST_H_AT)
         gelu(h3_low[:], 3, low)
         result3_low = second_layer(quantize(h3_low[:], "h3_low"), "h3_low")
-        h3_high = shared.tile([P, PACK * HALF], BF16, name="h3_high_bf", align_bytes=64, offset=LAST_H_AT + 1024)
+        h3_high = sb.tile([P, PACK * HALF], BF16, name="h3_high_bf", align_bytes=64)
         gelu(h3_high[:], 3, high)
         result3_high = second_layer(quantize(h3_high[:], "h3_high"), "h3_high")
 
         staged01 = shared.tile([N, 2 * CHUNK], F32, name="staged01", align_bytes=256, offset=LAST_H_AT - 768)
         nc.scalar.copy(staged01[:], result01[:])
         nc.sync.dma_start(out[:, : 2 * CHUNK], staged01[:])
-        staged2 = shared.tile([N, CHUNK], F32, name="staged2", align_bytes=256, offset=LAST_H_AT + 1024)
-        nc.vector.tensor_copy(staged2[:], result2[:])
+        staged2 = shared.tile([N, CHUNK], F32, name="staged2", align_bytes=256, offset=LAST_H_AT + 256)
+        nc.scalar.copy(staged2[:], result2[:])
         nc.sync.dma_start(out[:, 2 * CHUNK : 3 * CHUNK], staged2[:])
         staged3 = sb.tile([N, CHUNK], F32, name="staged3", align_bytes=256)
         nc.scalar.copy(staged3[:, low], result3_low[:])

from contextlib import ExitStack

import concourse.mybir as mybir

K, T, V, H, N, J = 1024, 2048, 512, 512, 128, 512
FLOPS = 2 * V * (2 * K * H + J * H + H * N)

F32 = mybir.dt.float32
BF16 = mybir.dt.bfloat16
I32 = mybir.dt.int32
U32 = mybir.dt.uint32
U16 = mybir.dt.uint16
U8 = mybir.dt.uint8
FP8X4 = mybir.dt.float8_e4m3fn_x4
GELU = mybir.ActivationFunctionType.Gelu_apprx_tanh

P = 128
PACK = 4
K_PASS = P * PACK
RUN = 4
QUADRANT = 32
CHUNK = 128
HALF = CHUNK // 2
N_CHUNKS = V // CHUNK
LIST = 2 * V

VECTOR_SHARE = (0, 0, 64, 80)
SECOND_VECTOR = 16
THIRD_VECTOR = 80

SCALE_TABLE_AT = 0
FIRST_CODES_AT = T - 64
W4_AT = 12288
LAST_H_AT = 16384


def tile_picked_edgeup_gelu_p_kernel(tc, x_words, x_scales, eT, w1, w2, w3, w4, offs, out):
    nc = tc.nc
    with ExitStack() as ctx:
        sb = ctx.enter_context(tc.tile_pool(name="sb", bufs=1))
        shared = ctx.enter_context(tc.tile_pool(name="shared", bufs=1))
        ps = ctx.enter_context(tc.psum_pool(name="ps", bufs=1))

        offsets = sb.tile([P, 2 * V // 16], U16, name="offsets", align_bytes=256)

        scale_table = shared.tile([P, T], U8, name="scale_table", align_bytes=256, offset=SCALE_TABLE_AT)
        nc.gpsimd.memset(scale_table[:].bitcast(I32), 0)
        x_planes = sb.tile([P, 2 * LIST], U8, name="x_planes", align_bytes=256)
        zero = sb.tile([P, 1], F32, name="zero")
        nc.gpsimd.memset(zero[:], 0.0)
        gelu_bias = sb.tile([P, 1], F32, name="gelu_bias")

        def load_rows(rows, name, at=None):
            pool = sb if at is None else shared
            raw = pool.tile([P, PACK, rows.shape[1]], F32, name=name, align_bytes=256, offset=at)
            nc.sync.dma_start(raw[:], rows.rearrange("(p j) c -> p j c", j=PACK))
            return raw

        def load_words(z):
            table = sb.tile([P, T], I32, name="word_table%d" % z, align_bytes=256)
            nc.sync.dma_start(table[:], x_words[z].rearrange("p n r -> p (n r)").bitcast(I32))
            return table

        word_tables = [load_words(0)]
        nc.sync.dma_start(offsets[:], offs)
        nc.sync.dma_start(scale_table[::PACK, :].bitcast(I32), x_scales.rearrange("z q n -> q z n").bitcast(I32))
        nc.scalar.activation(gelu_bias[:], zero[:], GELU)
        w_raw = [load_rows(w1[0:K_PASS, :], "w_raw0")]
        word_tables.append(load_words(1))
        w_raw.append(load_rows(w2[0:K_PASS, :], "w_raw1"))
        picked_scales = sb.tile([P, 2 * V], U8, name="picked_scales", align_bytes=256)
        nc.vector.tensor_copy(picked_scales[:], scale_table[:].indirect(offsets[:]))
        twice = picked_scales[:].bitcast(I32).unsqueeze(1).to_broadcast([P, 2, LIST // 4])
        nc.vector.tensor_copy(x_planes[:].bitcast(I32).rearrange("p (z n) -> p z n", z=2), twice)

        for z in range(2):
            for r in range(1, PACK):
                rows = picked_scales[PACK * z + 8 * r :: QUADRANT, :]
                place = x_planes[PACK * z + r :: QUADRANT, z * LIST : (z + 1) * LIST]
                queue = nc.gpsimd if (z, r) == (1, PACK - 1) else nc.sync
                queue.dma_start(place.bitcast(I32), rows.bitcast(I32))
        w_raw.append(load_rows(w1[K_PASS:K, :], "w_raw2"))
        w_raw.append(load_rows(w2[K_PASS:K, :], "w_raw3"))
        w3_raw = load_rows(w3, "w3_raw")

        e_raw = [load_rows(eT[:, c * CHUNK : (c + 1) * CHUNK], "e_raw%d" % c) for c in range(N_CHUNKS - 1)]
        early_rows, late_rows = slice(0, 2), slice(2, PACK)
        last_raw = sb.tile([P, PACK, CHUNK], F32, name="last_raw", align_bytes=256)
        last_rows = eT[:, V - CHUNK :].rearrange("(p j) c -> p j c", j=PACK)
        for rows in (early_rows, late_rows):
            nc.sync.dma_start(last_raw[:, rows, :], last_rows[:, rows, :])
        w4_raw = load_rows(w4, "w4_raw", W4_AT)

        x_codes = [
            shared.tile([P, 2 * V], U32, name="x_codes0", align_bytes=64, offset=FIRST_CODES_AT),
            sb.tile([P, 2 * V], U32, name="x_codes1", align_bytes=64),
        ]
        for z in range(2):
            nc.vector.tensor_copy(x_codes[z][:], word_tables[z][:].bitcast(U32).indirect(offsets[:]))

        def quantize(values, name, at=None):
            width = values.shape[1] // PACK
            pool = sb if at is None else shared
            codes = pool.tile([P, width], U32, name=name + "_codes", align_bytes=64, offset=at)
            plane = sb.tile([P, width], U8, name=name + "_plane", align_bytes=64)
            nc.vector.quantize_mx(codes[:].bitcast(FP8X4), plane[:], values)
            return codes, plane

        def multiply(result, weights, w_cols, codes, plane, start, stop):
            nc.tensor.matmul_mx(
                result,
                lhsT=weights[0][:, w_cols].bitcast(FP8X4),
                lhsT_scale=weights[1][:, w_cols],
                rhs=codes.bitcast(FP8X4),
                rhs_scale=plane,
                start=start,
                stop=stop,
            )

        def round_dealt(raw, share, name):
            grouped = sb.tile([P, PACK * H], BF16, name=name, align_bytes=64)
            dst = grouped[:].rearrange("p (t m j) -> p m j t", t=PACK, j=PACK)
            src = raw[:].rearrange("p j (m t) -> p m j t", t=PACK)
            if share > 0:
                nc.vector.tensor_copy(dst[:, :share], src[:, :share])
            nc.scalar.copy(dst[:, share:], src[:, share:])
            return grouped

        def round_plain(raw, grouped, copy, rows=slice(0, PACK)):
            dst = grouped[:].rearrange("p (c e j) -> p c j e", e=RUN, j=PACK)
            copy(dst[:, :, rows, :], raw[:, rows, :].rearrange("p j (c e) -> p c j e", e=RUN))

        tile_cols = [slice(t * P, (t + 1) * P) for t in range(PACK)]
        whole, low, high = slice(0, CHUNK), slice(0, HALF), slice(HALF, CHUNK)

        hidden = [ps.tile([P, PACK, CHUNK], F32, name="hidden%d" % c) for c in range(N_CHUNKS)]
        for g in range(4):
            z, side = divmod(g, 2)
            w_mx = quantize(round_dealt(w_raw[g], VECTOR_SHARE[g], "w_bf%d" % g)[:], "w%d" % g)
            for t in range(PACK):
                for c in range(N_CHUNKS):
                    entries = slice(side * V + c * CHUNK, side * V + (c + 1) * CHUNK)
                    plane = x_planes[PACK * z :, z * LIST + entries.start : z * LIST + entries.stop]
                    multiply(hidden[c][:, t, :], w_mx, tile_cols[t], x_codes[z][:, entries], plane, g == 0 and t == 0, False)

        def round_pair(pair, copy):
            grouped = sb.tile([P, 2 * K_PASS], BF16, name="w3_bf%d" % pair, align_bytes=64)
            src = w3_raw[:].rearrange("p j (m t) -> p m j t", t=PACK)[:, :, :, 2 * pair : 2 * pair + 2]
            copy(grouped[:].rearrange("p (t m j) -> p m j t", t=2, j=PACK), src)
            return grouped

        e_bf = [sb.tile([P, K_PASS], BF16, name="e_bf%d" % c, align_bytes=64) for c in range(N_CHUNKS - 1)]

        def round_edges(c, cols, copy):
            round_plain(e_raw[c][:, :, cols], e_bf[c][:, PACK * cols.start : PACK * cols.stop], copy)

        def edge_pass(c, e_mx):
            for t in range(PACK):
                multiply(hidden[c][:, t, :], w3_mx[t // 2], tile_cols[t % 2], e_mx[0][:], e_mx[1][:], False, t == PACK - 1)

        w3_bf = [round_pair(0, nc.vector.tensor_copy), round_pair(1, nc.scalar.copy)]
        round_edges(0, whole, nc.vector.tensor_copy)
        w3_mx = [quantize(w3_bf[0][:], "w3_0")]
        e_mx = quantize(e_bf[0][:], "e0")
        round_edges(1, slice(0, SECOND_VECTOR), nc.vector.tensor_copy)
        round_edges(1, slice(SECOND_VECTOR, CHUNK), nc.scalar.copy)
        w3_mx.append(quantize(w3_bf[1][:], "w3_1"))
        edge_pass(0, e_mx)
        edge_pass(1, quantize(e_bf[1][:], "e1"))
        round_edges(2, slice(0, THIRD_VECTOR), nc.vector.tensor_copy)
        round_edges(2, slice(THIRD_VECTOR, CHUNK), nc.scalar.copy)
        last_bf = sb.tile([P, K_PASS], BF16, name="last_bf", align_bytes=64)
        round_plain(last_raw, last_bf, nc.vector.tensor_copy, early_rows)
        edge_pass(2, quantize(e_bf[2][:], "e2"))
        last_values = [last_bf[:, PACK * half.start : PACK * half.stop] for half in (low, high)]
        last_mx = (
            sb.tile([P, CHUNK], U32, name="e3_codes", align_bytes=64),
            sb.tile([P, CHUNK], U8, name="e3_plane", align_bytes=64),
        )
        for values, half in zip(last_values, (low, high)):
            round_plain(last_raw[:, :, half], values, nc.vector.tensor_copy, late_rows)
        for values, half in zip(last_values, (low, high)):
            nc.vector.quantize_mx(last_mx[0][:, half].bitcast(FP8X4), last_mx[1][:, half], values[:])
        edge_pass(3, last_mx)

        w4_bf = sb.tile([P, PACK * N], BF16, name="w4_bf", align_bytes=64)
        round_plain(w4_raw, w4_bf, nc.vector.tensor_copy)
        w4_mx = quantize(w4_bf[:], "w4")

        def gelu(h_bf, c, cols):
            nc.scalar.activation(
                h_bf.rearrange("p (v t) -> p v t", t=PACK),
                hidden[c][:, :, cols].rearrange("p t v -> p v t"),
                GELU,
                bias=gelu_bias[:],
            )

        def second_layer(h_mx, name):
            result = ps.tile([N, h_mx[0].shape[1]], F32, name=name + "_result")
            multiply(result[:], w4_mx, slice(0, N), h_mx[0][:], h_mx[1][:], True, True)
            return result

        h01 = sb.tile([P, 2 * K_PASS], BF16, name="h01_bf", align_bytes=64)
        for c in range(2):
            gelu(h01[:, c * K_PASS : (c + 1) * K_PASS], c, whole)
        h01_mx = quantize(h01[:], "h01", W4_AT)
        result01 = second_layer(h01_mx, "h01")
        h2 = sb.tile([P, K_PASS], BF16, name="h2_bf", align_bytes=64)
        gelu(h2[:], 2, whole)
        result2 = second_layer(quantize(h2[:], "h2", W4_AT + 1024), "h2")
        h3_low = shared.tile([P, PACK * HALF], BF16, name="h3_low_bf", align_bytes=64, offset=LAST_H_AT)
        gelu(h3_low[:], 3, low)
        result3_low = second_layer(quantize(h3_low[:], "h3_low"), "h3_low")
        h3_high = sb.tile([P, PACK * HALF], BF16, name="h3_high_bf", align_bytes=64)
        gelu(h3_high[:], 3, high)
        result3_high = second_layer(quantize(h3_high[:], "h3_high"), "h3_high")

        staged01 = shared.tile([N, 2 * CHUNK], F32, name="staged01", align_bytes=256, offset=LAST_H_AT - 768)
        nc.scalar.copy(staged01[:], result01[:])
        nc.sync.dma_start(out[:, : 2 * CHUNK], staged01[:])
        staged2 = shared.tile([N, CHUNK], F32, name="staged2", align_bytes=256, offset=LAST_H_AT + 256)
        nc.scalar.copy(staged2[:], result2[:])
        nc.sync.dma_start(out[:, 2 * CHUNK : 3 * CHUNK], staged2[:])
        staged3 = sb.tile([N, CHUNK], F32, name="staged3", align_bytes=256)
        nc.scalar.copy(staged3[:, low], result3_low[:])
        nc.vector.tensor_copy(staged3[:, high], result3_high[:])
        nc.sync.dma_start(out[:, 3 * CHUNK :], staged3[:])
